import numpy as np
import ml_dtypes


def mxq(x, axis, fmt="e4m3"):
    dtype, down = {"e4m3": (ml_dtypes.float8_e4m3fn, 7), "e5m2": (ml_dtypes.float8_e5m2, 14)}[fmt]
    v = np.moveaxis(np.asarray(x, np.float32).astype(ml_dtypes.bfloat16).astype(np.float64), axis, -1)
    blocks = v.reshape(v.shape[:-1] + (-1, 32))
    amax = np.abs(blocks).max(-1, keepdims=True)
    byte = np.maximum(np.where(amax > 0, np.frexp(amax)[1] - 1 + 127, 0) - down, 1)
    scale = np.exp2(byte - 127.0)
    codes = (blocks / scale).astype(np.float32).astype(dtype).astype(np.float64)
    return np.moveaxis((codes * scale).reshape(v.shape), -1, axis)


WIDE = False


def mx_kscale(k):
    if not WIDE:
        return np.ones(k)
    levels = np.array([10, -10, 5, -5, 0])
    if k % 512:
        return np.exp2(np.random.permutation(np.resize(levels, k // 32))).repeat(32)
    a = np.empty((k // 512, 16))
    for p in range(k // 512):
        a[p, :8] = np.random.permutation(np.resize(levels, 8))
        for g in range(8):
            far = levels[np.abs(levels - a[p, g]) >= 10]
            a[p, g + 8] = far[np.random.randint(len(far))]
    return np.exp2(a.ravel()).repeat(32)


def f64(x):
    return np.asarray(x).astype(np.float64)


def striped(idx):
    return np.tile(idx.reshape(-1, 16).T, (8, 1)).astype(np.uint16)


def unstriped(offs):
    return offs[:16].T.reshape(-1).astype(np.int64)


E2M1 = np.array([0.0, 0.5, 1.0, 1.5, 2.0, 3.0, 4.0, 6.0, -0.0, -0.5, -1.0, -1.5, -2.0, -3.0, -4.0, -6.0])


def pack_weight(w, fmt):
    k, n = w.shape
    w = f64(np.asarray(w, np.float32).astype(ml_dtypes.bfloat16)).reshape(k // 32, 32, n)
    amax = np.abs(w).max(1)
    if fmt == "e4m3":
        byte = np.frexp(amax)[1] - 1 + 127 - 7
    else:
        mant, ex = np.frexp(amax / 6.0)
        byte = np.where(mant > 0.5, ex, ex - 1) + 127
    byte = np.clip(np.where(amax > 0, byte, 1), 1, 254)
    scaled = (w * np.exp2(127.0 - byte)[:, None, :]).reshape(k, n).astype(np.float32)
    by_word = np.ascontiguousarray(scaled.reshape(k // 512, 128, 4, n).transpose(0, 1, 3, 2))
    if fmt == "e4m3":
        words = by_word.astype(ml_dtypes.float8_e4m3fn).view(np.uint8)
    else:
        c = by_word.astype(ml_dtypes.float4_e2m1fn).view(np.uint8) & 0xF
        words = (c[..., 0::2] | (c[..., 1::2] << 4)).reshape(k // 512, 128, 2 * n)
    return np.ascontiguousarray(words), np.ascontiguousarray(byte.astype(np.uint8).reshape(k // 512, 16, n))


def unpack_weight(words, scales, fmt):
    g, _, n = scales.shape
    words = np.ascontiguousarray(words).reshape(g, 128, n, -1)
    if fmt == "e4m3":
        vals = words.view(ml_dtypes.float8_e4m3fn).astype(np.float64)
    else:
        nib = np.empty((g, 128, n, 4), np.uint8)
        nib[..., 0::2] = words & 0xF
        nib[..., 1::2] = words >> 4
        vals = E2M1[nib]
    vals = vals * np.repeat(np.exp2(scales.astype(np.float64) - 127.0), 8, axis=1)[..., None]
    return vals.transpose(0, 1, 3, 2).reshape(g * 512, n)


def gelu(v):
    return 0.5 * v * (1.0 + np.tanh(np.sqrt(2.0 / np.pi) * (v + 0.044715 * v**3)))


def bf(x):
    return np.asarray(x, np.float32).astype(ml_dtypes.bfloat16)


def planes(Y):
    n, m = Y.shape
    b = f64(bf(Y)).reshape(n // 32, 32, m)
    amax = np.abs(b).max(1)
    byte = np.clip(np.where(amax > 0, np.frexp(amax)[1] - 1 + 127 - 7, 1), 1, 254)
    codes = (b * np.exp2(127.0 - byte)[:, None, :]).reshape(n, m).astype(np.float32).astype(ml_dtypes.float8_e4m3fn).view(np.uint8)
    words = codes.reshape(n // 512, 128, 4, m).transpose(0, 1, 3, 2)
    return np.ascontiguousarray(words), np.ascontiguousarray(byte.astype(np.uint8).reshape(n // 512, 16, m))


K, K2, H, N, T, T2, S, P = 512, 1024, 1024, 512, 2048, 1024, 1024, 512


def setup_inputs():
    n = np.random.standard_normal
    s = mx_kscale(K)[:, None]
    s2 = mx_kscale(K2)[:, None]
    u = mx_kscale(H)[:, None]
    d = {}
    d["tab_words"], d["tab_scales"] = pack_weight(n((K, T)) * s, "e4m3")
    d["tab2_words"], d["tab2_scales"] = pack_weight(n((K2, T2)) * s2, "e4m3")
    d["offs"] = striped(np.random.permutation(T)[:S])
    d["offs2"] = striped(np.random.permutation(T2)[:P])
    d["pos1"] = striped(np.random.permutation(S)[:P])
    d["wa"] = (0.5 * n((K, H)) / K**0.5 / s).astype(np.float32)
    d["ws_words"], d["ws_scales"] = pack_weight(0.55 * n((K, H)) / K**0.5 / s, "e2m1")
    d["wb"] = (n((K2, H)) / K2**0.5 / s2).astype(np.float32)
    d["gb"] = np.exp(0.3 * n(H)).astype(np.float32)
    d["wgs"] = np.exp(0.3 * n((128, P))).astype(np.float32)
    d["gz"] = (np.exp(0.3 * n(H)) * u[:, 0]).astype(np.float32)
    wo = 2.0 * n((H, N)) / H**0.5 * np.exp(0.8 * n(N))[None, :] / u
    d["wo_words"], d["wo_scales"] = pack_weight(wo, "e4m3")
    return d


def reference(tab_words, tab_scales, tab2_words, tab2_scales, offs, offs2, pos1, wa, ws_words, ws_scales, wb, gb, wgs, gz, wo_words, wo_scales):
    v = unpack_weight(tab_words, tab_scales, "e4m3")[:, unstriped(offs)]
    v2 = unpack_weight(tab2_words, tab2_scales, "e4m3")[:, unstriped(offs2)]
    ws = unpack_weight(ws_words, ws_scales, "e2m1")
    wo = unpack_weight(wo_words, wo_scales, "e4m3")
    a = (mxq(f64(wa), 0, "e4m3").T @ v) + np.sin(ws.T @ v)
    b = (mxq(f64(wb), 0, "e4m3").T @ v2) * f64(gb)[:, None]
    placed = np.zeros((H, S))
    placed[:, unstriped(pos1)] = np.tile(f64(wgs), (H // 128, 1)) * b
    z = f64(gz)[:, None] * (a + placed) / (1.0 + np.abs(placed))
    y = wo.T @ mxq(z, 0, "e4m3")
    words, scales = planes(y)
    return y, words, scales

@@ -1,0 +1,313 @@
+import math
+from contextlib import ExitStack
+
+import concourse.mybir as mybir
+from concourse.masks import make_identity
+
+K, K2, H, N, T, T2, S, NP = 512, 1024, 1024, 512, 2048, 1024, 1024, 512
+FLOPS = 2 * (2 * K * H * S + K2 * H * NP + H * N * S)
+
+F32 = mybir.dt.float32
+BF16 = mybir.dt.bfloat16
+I32 = mybir.dt.int32
+U32 = mybir.dt.uint32
+U16 = mybir.dt.uint16
+U8 = mybir.dt.uint8
+FP8X4 = mybir.dt.float8_e4m3fn_x4
+FP4X4 = mybir.dt.float4_e2m1fn_x4
+ALU = mybir.AluOpType
+ACT = mybir.ActivationFunctionType
+
+P = 128
+BANK = 512
+TWO_PI = 2.0 * math.pi
+CHUNKS = [(0, 512), (512, 256), (768, 256)]
+
+
+def tile_list_mushroom_flush_features_kernel(
+    tc, tab_words, tab_scales, tab2_words, tab2_scales, offs, offs2, pos1, wa, ws_words, ws_scales,
+    wb, gb, wgs, gz, wo_words, wo_scales, out_0, out_1, out_2,
+):
+    nc = tc.nc
+    with ExitStack() as ctx:
+        keep = ctx.enter_context(tc.tile_pool(name="keep", bufs=1))
+        big = ctx.enter_context(tc.tile_pool(name="big", bufs=8))
+        half = ctx.enter_context(tc.tile_pool(name="half", bufs=3))
+        turns = ctx.enter_context(tc.tile_pool(name="turns", bufs=3))
+        bpool = ctx.enter_context(tc.tile_pool(name="bpool", bufs=5))
+        ps_s = ctx.enter_context(tc.psum_pool(name="ps_s", bufs=3))
+        ps_m = ctx.enter_context(tc.psum_pool(name="ps_m", bufs=2))
+        ps_t = ctx.enter_context(tc.psum_pool(name="ps_t", bufs=3))
+
+        def kept(shape, dtype, name):
+            return keep.tile(shape, dtype, name=name, align_bytes=64)
+
+        def big_tile(shape, dtype, name):
+            return big.tile(shape, dtype, name=name, tag="big", align_bytes=64)
+
+        def zeroed_plane(width, name):
+            plane = kept([P, width], U8, name)
+            nc.vector.memset(plane[:].bitcast(I32), 0)
+            return plane
+
+        def load_planes(plane, scales):
+            passes = scales.shape[0]
+            for q in range(4):
+                nc.sync.dma_start(
+                    out=plane[32 * q : 32 * q + 4 * passes, :].bitcast(I32),
+                    in_=scales[:, 4 * q : 4 * q + 4, :].bitcast(I32),
+                )
+
+        idx = keep.tile([P, S // 16], U16, name="idx")
+        idx2 = keep.tile([P, NP // 16], U16, name="idx2")
+        place = keep.tile([P, NP // 16], U16, name="place")
+
+        tab_s = zeroed_plane(T, "tab_s")
+        ws_s = zeroed_plane(H, "ws_s")
+        tab2_s = zeroed_plane(T2, "tab2_s")
+        wo_s = zeroed_plane(N, "wo_s")
+        pages = [kept([P, S], F32, f"page{i}") for i in range(4)]
+        for page in pages:
+            nc.vector.memset(page[:], 0.0)
+        ident = kept([P, P], F32, "ident")
+        make_identity(nc, ident[:])
+
+        gb_t = kept([P, 2, 4], F32, "gb_t")
+        gz_t = kept([P, 2, 4], F32, "gz_t")
+        nc.sync.dma_start(idx[:], offs)
+        nc.sync.dma_start(idx2[:], offs2)
+        nc.sync.dma_start(place[:], pos1)
+        nc.sync.dma_start(out=gb_t[:], in_=gb.rearrange("(b p t) -> p b t", b=2, t=4))
+        tab_w = big_tile([P, T], I32, "tab_w")
+        tab_rows = tab_words[0].rearrange("p t i -> p (t i)").bitcast(I32)
+        for h in range(2):
+            cols = slice(h * T // 2, (h + 1) * T // 2)
+            nc.sync.dma_start(out=tab_w[:, cols], in_=tab_rows[:, cols])
+        ws_w = kept([P, 2 * H], U8, "ws_w")
+        nc.sync.dma_start(out=ws_w[:].bitcast(I32), in_=ws_words[0].bitcast(I32))
+        nc.sync.dma_start(out=gz_t[:], in_=gz.rearrange("(b p t) -> p b t", b=2, t=4))
+        load_planes(tab_s, tab_scales)
+        load_planes(ws_s, ws_scales)
+
+        def load_weight(w, a, b, name):
+            raw = big_tile([P, 4, BANK], F32, name)
+            rows = w[a * 512 : (a + 1) * 512, b * 512 : (b + 1) * 512]
+            nc.sync.dma_start(out=raw[:], in_=rows.rearrange("(p j) c -> p j c", j=4))
+            return raw
+
+        wb_raw = {(a, 0): load_weight(wb, a, 0, f"wb_raw{a}0") for a in range(2)}
+        tab2_w = big_tile([P, 2, T2], I32, "tab2_w")
+        nc.sync.dma_start(out=tab2_w[:], in_=tab2_words.rearrange("a p t i -> p a (t i)").bitcast(I32))
+        load_planes(tab2_s, tab2_scales)
+        wa_raw = [load_weight(wa, 0, b, f"wa_raw{b}") for b in range(2)]
+        wg = kept([P, 4, NP], F32, "wg")
+        for q in range(4):
+            nc.sync.dma_start(out=wg[32 * q : 32 * q + 32], in_=wgs.rearrange("(m t) j -> m t j", t=4))
+        wb_raw = {**wb_raw, **{(a, 1): load_weight(wb, a, 1, f"wb_raw{a}1") for a in range(2)}}
+        wo_w = kept([P, 2, N], I32, "wo_w")
+        nc.sync.dma_start(out=wo_w[:], in_=wo_words.rearrange("a p c i -> p a (c i)").bitcast(I32))
+        load_planes(wo_s, wo_scales)
+
+        v_w = kept([P, S], U32, "v_w")
+        v_s = kept([P, S], U8, "v_s")
+        nc.vector.tensor_copy(v_w[:], tab_w[:].bitcast(U32).indirect(idx[:]))
+        for h in range(2):
+            cols = slice(h * 512, (h + 1) * 512)
+            nc.vector.tensor_copy(v_s[:, cols], tab_s[:].indirect(idx[:, h * 32 : (h + 1) * 32]))
+
+        def quantise_weight(raw, name):
+            grouped = half.tile([P, 4 * BANK], BF16, name="grouped", tag="half", align_bytes=64)
+            nc.scalar.copy(
+                grouped[:].rearrange("p (u v m j) -> p u m j v", u=2, v=2, j=4),
+                raw[:].rearrange("p j (m u v) -> p u m j v", u=2, v=2),
+            )
+            codes = kept([P, BANK], U32, name + "_w")
+            scales = kept([P, BANK], U8, name + "_s")
+            nc.vector.quantize_mx(out=codes[:].bitcast(FP8X4), scales=scales[:], in_=grouped[:])
+            return codes, scales
+
+        sn = [kept([P, H], F32, f"sn{jb}") for jb in range(8)]
+        at = [kept([P, H], F32, f"at{jb}") for jb in range(8)]
+
+        def sine_front(i):
+            jb, b = divmod(i, 2)
+            js = slice(jb * P, (jb + 1) * P)
+            bank = ps_s.tile([P, BANK], F32, name="s_bank")
+            nc.tensor.matmul_mx(
+                out=bank[:], lhsT=v_w[:, js].bitcast(FP8X4), lhsT_scale=v_s[:, js],
+                rhs=ws_w[:, 2 * b * BANK : 2 * (b + 1) * BANK].bitcast(FP4X4),
+                rhs_scale=ws_s[:, b * BANK : (b + 1) * BANK], start=True, stop=True,
+            )
+            dealt = bank[:].rearrange("p (q t) -> p t q", t=4)
+            k = turns.tile([P, 4, P], I32, name="k")
+            nc.vector.tensor_scalar(k[:], dealt, 1.0 / TWO_PI, None, ALU.mult)
+            return dealt, k
+
+        def sine_back(i, dealt, k):
+            jb, b = divmod(i, 2)
+            dst = sn[jb][:, b * BANK : (b + 1) * BANK]
+            nc.vector.scalar_tensor_tensor(
+                dst.rearrange("p (t q) -> p t q", t=4), k[:], -TWO_PI, dealt, ALU.mult, ALU.add
+            )
+            nc.scalar.activation(dst, dst, ACT.Sin)
+
+        todo = [("wb", 0, 0), ("wb", 1, 0), ("wa", 0, 0), ("wa", 0, 1), ("wb", 0, 1), ("wb", 1, 1)]
+        w_q = {}
+        front = sine_front(0)
+        for i in range(16):
+            nxt = sine_front(i + 1) if i + 1 < 16 else None
+            sine_back(i, *front)
+            front = nxt
+            if i % 2 == 1 and i // 2 < 6:
+                name, a, b = todo[i // 2]
+                raw = wb_raw[a, b] if name == "wb" else wa_raw[b]
+                w_q[name, a, b] = quantise_weight(raw, f"{name}{a}{b}")
+        wa_q = [w_q["wa", 0, b] for b in range(2)]
+        wb_q = {(a, b): w_q["wb", a, b] for a in range(2) for b in range(2)}
+
+        sg = kept([P, 8], F32, "sg")
+        inv = kept([P, 8], F32, "inv")
+        mag = kept([P, 8], F32, "mag")
+        gbs = kept([P, 8], F32, "gbs")
+        gz_f = gz_t[:].rearrange("p b t -> p (b t)")
+        nc.scalar.activation(sg[:], gz_f, ACT.Sign)
+        nc.vector.tensor_tensor(mag[:], gz_f, sg[:], ALU.mult)
+        nc.vector.tensor_tensor(gbs[:], gb_t[:].rearrange("p b t -> p (b t)"), sg[:], ALU.mult)
+        nc.vector.tensor_scalar_max(mag[:], mag[:], 1e-30)
+        nc.vector.reciprocal(inv[:], mag[:])
+
+        v2_w = kept([P, 2, NP], U32, "v2_w")
+        v2_s = kept([P, NP], U8, "v2_s")
+        for a in range(2):
+            nc.vector.tensor_copy(v2_w[:, a, :], tab2_w[:, a, :].bitcast(U32).indirect(idx2[:]))
+        nc.vector.tensor_copy(v2_s[:], tab2_s[:].indirect(idx2[:]))
+
+        def short_product(s):
+            b, t = divmod(s, 4)
+            ms = slice(t * P, (t + 1) * P)
+            bank = ps_m.tile([P, BANK], F32, name="b_bank", tag="m")
+            for a in range(2):
+                codes, scales = wb_q[a, b]
+                nc.tensor.matmul_mx(
+                    out=bank[:], lhsT=codes[:, ms].bitcast(FP8X4), lhsT_scale=scales[:, ms],
+                    rhs=v2_w[:, a, :].bitcast(FP8X4), rhs_scale=v2_s[4 * a : P, :],
+                    start=(a == 0), stop=(a == 1),
+                )
+            bsb = bpool.tile([P, NP], F32, name="bsb")
+            nc.scalar.activation(bsb[:], bank[:], ACT.Copy, scale=gbs[:, s : s + 1])
+            return bsb
+
+        damp = {}
+        numer = {}
+
+        def damping(s):
+            b, t = divmod(s, 4)
+            for h in range(2):
+                if t == 0:
+                    damp[b, h] = big_tile([P, 4, BANK], F32, f"damp{b}{h}")
+                dst = damp[b, h][:, t, :]
+                nc.scalar.activation(dst, pages[s % 4][:, h * BANK : (h + 1) * BANK], ACT.Abs)
+            for h in range(2):
+                dst = damp[b, h][:, t, :]
+                nc.scalar.activation(
+                    dst, dst, ACT.Abs_reciprocal_sqrt, scale=inv[:, s : s + 1], bias=inv[:, s : s + 1]
+                )
+            for h in range(2):
+                dst = damp[b, h][:, t, :]
+                nc.scalar.activation(dst, dst, ACT.Square)
+
+        def numerator(s):
+            b, t = divmod(s, 4)
+            rs = slice(s * P, (s + 1) * P)
+            for h in range(2):
+                if t == 0:
+                    numer[b, h] = big_tile([P, 4, BANK], F32, f"numer{b}{h}")
+                bank = ps_t.tile([P, BANK], F32, name="sum_bank", tag="t")
+                for c in range(4):
+                    dst = bank[:, c * P : (c + 1) * P]
+                    jb = 4 * h + c
+                    nc.tensor.matmul(dst, sn[jb][:, rs], ident[:], start=True, stop=False, is_transpose=True)
+                    nc.tensor.matmul(dst, at[jb][:, rs], ident[:], start=False, stop=True, is_transpose=True)
+                nc.vector.scalar_tensor_tensor(
+                    numer[b, h][:, t, :], bank[:], sg[:, s : s + 1],
+                    pages[s % 4][:, h * BANK : (h + 1) * BANK], ALU.mult, ALU.add,
+                )
+
+        short = [short_product(s) for s in range(4)]
+
+        for jb in range(8):
+            js = slice(jb * P, (jb + 1) * P)
+            for b in range(2):
+                bank = ps_m.tile([P, BANK], F32, name="a_bank", tag="m")
+                nc.tensor.matmul_mx(
+                    out=bank[:], lhsT=v_w[:, js].bitcast(FP8X4), lhsT_scale=v_s[:, js],
+                    rhs=wa_q[b][0][:].bitcast(FP8X4), rhs_scale=wa_q[b][1][:], start=True, stop=True,
+                )
+                nc.scalar.copy(at[jb][:, b * BANK : (b + 1) * BANK], bank[:])
+
+        wo_dw = kept([P, 2, N], I32, "wo_dw")
+        wo_ds = kept([P, N], U8, "wo_ds")
+        nc.vector.tensor_copy(
+            wo_dw[:].rearrange("p a (u v m) -> p a u m v", u=2, v=2),
+            wo_w[:].rearrange("p a (m u v) -> p a u m v", u=2, v=2),
+        )
+        nc.vector.tensor_copy(
+            wo_ds[:].rearrange("p (t m) -> p t m", t=4), wo_s[:].rearrange("p (m t) -> p t m", t=4)
+        )
+
+        for s in range(8):
+            nc.vector.tensor_tensor(pages[s % 4][:].indirect(place[:]), short[s][:], wg[:, s % 4, :], ALU.mult)
+            if s + 4 < 8:
+                short.append(short_product(s + 4))
+            damping(s)
+            if s >= 2:
+                numerator(s - 2)
+        numerator(6)
+        numerator(7)
+
+        z_w = [kept([P, S], U32, f"z_w{b}") for b in range(2)]
+        z_s = [kept([P, S], U8, f"z_s{b}") for b in range(2)]
+        y_w = kept([P, S], I32, "y_w")
+        y_s = kept([P, S], U8, "y_s")
+        y_rows = out_0.rearrange("(p t) j -> p t j", t=4)
+        y_codes = out_1[0].rearrange("p m t -> p (m t)").bitcast(I32)
+        for c0, width in CHUNKS:
+            h, off = divmod(c0, BANK)
+            cols = slice(c0, c0 + width)
+            for b in range(2):
+                zb = half.tile([P, 4 * width], BF16, name="zb", tag="half", align_bytes=64)
+                nc.vector.tensor_tensor(
+                    zb[:].rearrange("p (c i t) -> p c t i", i=2, t=4),
+                    numer[b, h][:, :, off : off + width].rearrange("p t (c i) -> p c t i", i=2),
+                    damp[b, h][:, :, off : off + width].rearrange("p t (c i) -> p c t i", i=2),
+                    ALU.mult,
+                )
+                nc.vector.quantize_mx(out=z_w[b][:, cols].bitcast(FP8X4), scales=z_s[b][:, cols], in_=zb[:])
+            ysb = big_tile([P, 4, width], F32, "ysb")
+            yb = half.tile([P, width, 4], BF16, name="yb", tag="half", align_bytes=64)
+            for c in range(width // P):
+                js = slice(c0 + c * P, c0 + (c + 1) * P)
+                bank = ps_t.tile([P, 4, P], F32, name="y_bank", tag="t")
+                for t in range(4):
+                    ms = slice(t * P, (t + 1) * P)
+                    for b in range(2):
+                        nc.tensor.matmul_mx(
+                            out=bank[:, t, :], lhsT=wo_dw[:, b, ms].bitcast(FP8X4), lhsT_scale=wo_ds[4 * b : P, ms],
+                            rhs=z_w[b][:, js].bitcast(FP8X4), rhs_scale=z_s[b][:, js],
+                            start=(b == 0), stop=(b == 1),
+                        )
+                woven = bank[:].rearrange("p t n -> p n t")
+                if c0 + width == S:
+                    nc.vector.tensor_copy(yb[:, c * P : (c + 1) * P, :], woven)
+                else:
+                    nc.scalar.copy(yb[:, c * P : (c + 1) * P, :], woven)
+                nc.scalar.copy(ysb[:, :, c * P : (c + 1) * P], bank[:])
+            nc.vector.quantize_mx(
+                out=y_w[:, cols].bitcast(FP8X4), scales=y_s[:, cols], in_=yb[:].rearrange("p n t -> p (n t)")
+            )
+            nc.sync.dma_start(out=y_rows[:, :, cols], in_=ysb[:])
+            nc.sync.dma_start(out=y_codes[:, cols], in_=y_w[:, cols])
+        for q in range(4):
+            nc.sync.dma_start(
+                out=out_2[0, 4 * q : 4 * q + 4, :].bitcast(I32), in_=y_s[32 * q : 32 * q + 4, :].bitcast(I32)
+            )

@@ -21,7 +21,7 @@ ACT = mybir.ActivationFunctionType
 P = 128
 BANK = 512
 TWO_PI = 2.0 * math.pi
-CHUNKS = [(0, 512), (512, 256), (768, 256)]
+CHUNKS = [(0, 256), (256, 256), (512, 256), (768, 128), (896, 128)]
 
 
 def tile_list_mushroom_flush_features_kernel(
@@ -31,19 +31,27 @@ def tile_list_mushroom_flush_features_kernel(
     nc = tc.nc
     with ExitStack() as ctx:
         keep = ctx.enter_context(tc.tile_pool(name="keep", bufs=1))
-        big = ctx.enter_context(tc.tile_pool(name="big", bufs=8))
-        half = ctx.enter_context(tc.tile_pool(name="half", bufs=3))
-        turns = ctx.enter_context(tc.tile_pool(name="turns", bufs=3))
-        bpool = ctx.enter_context(tc.tile_pool(name="bpool", bufs=5))
-        ps_s = ctx.enter_context(tc.psum_pool(name="ps_s", bufs=3))
-        ps_m = ctx.enter_context(tc.psum_pool(name="ps_m", bufs=2))
-        ps_t = ctx.enter_context(tc.psum_pool(name="ps_t", bufs=3))
+        psum = ctx.enter_context(tc.psum_pool(name="psum", bufs=1))
 
-        def kept(shape, dtype, name):
-            return keep.tile(shape, dtype, name=name, align_bytes=64)
+        def kept(shape, dtype, name, tag=None):
+            return keep.tile(shape, dtype, name=name, tag=tag or name, align_bytes=64)
 
-        def big_tile(shape, dtype, name):
-            return big.tile(shape, dtype, name=name, tag="big", align_bytes=64)
+        banks = [psum.tile([P, BANK], F32, name=f"bank{i}") for i in range(8)]
+        m_banks = banks[0:2]
+        s_banks = banks[2:5]
+        t_banks = [banks[i] for i in (2, 1, 0, 4, 3, 5, 6, 7)]
+        y_banks = banks[0:5]
+        wide_tiles = [kept([P, 4 * BANK], F32, f"wide{i}") for i in range(8)]
+        wide = [tile[:].rearrange("p (a c) -> p a c", a=4) for tile in wide_tiles]
+        at = [kept([P, H], F32, f"at{jb}") for jb in range(8)]
+        staging = [kept([P, 4 * BANK], BF16, f"staging{i}") for i in range(3)]
+        turns = [kept([P, 4, P], I32, f"turns{i}") for i in range(3)]
+        used = {}
+
+        def take(name, tiles):
+            n = used.setdefault(name, [])
+            n.append(0)
+            return tiles[(len(n) - 1) % len(tiles)]
 
         def zeroed_plane(width, name):
             plane = kept([P, width], U8, name)
@@ -58,89 +66,151 @@ def tile_list_mushroom_flush_features_kernel(
                     in_=scales[:, 4 * q : 4 * q + 4, :].bitcast(I32),
                 )
 
+        def load_weight(w, a, b, raw):
+            rows = w[a * 512 : (a + 1) * 512, b * 512 : (b + 1) * 512]
+            nc.sync.dma_start(out=raw, in_=rows.rearrange("(p j) c -> p j c", j=4))
+            return raw
+
         idx = keep.tile([P, S // 16], U16, name="idx")
         idx2 = keep.tile([P, NP // 16], U16, name="idx2")
         place = keep.tile([P, NP // 16], U16, name="place")
 
+        tab2_s = zeroed_plane(T2, "tab2_s")
         tab_s = zeroed_plane(T, "tab_s")
         ws_s = zeroed_plane(H, "ws_s")
-        tab2_s = zeroed_plane(T2, "tab2_s")
         wo_s = zeroed_plane(N, "wo_s")
         pages = [kept([P, S], F32, f"page{i}") for i in range(4)]
-        for page in pages:
+        for i, page in enumerate(pages):
             nc.vector.memset(page[:], 0.0)
         ident = kept([P, P], F32, "ident")
         make_identity(nc, ident[:])
 
         gb_t = kept([P, 2, 4], F32, "gb_t")
         gz_t = kept([P, 2, 4], F32, "gz_t")
+        tab2_w = kept([P, 2, T2], I32, "tab2_w", "table2_then_y")
+        tab_w = kept([P, T], I32, "tab_w", "table_then_y")
+        wg = kept([P, 4, NP], F32, "wg")
+        ws_w = kept([P, 2 * H], U8, "ws_w")
+        wo_w = kept([P, 2, N], I32, "wo_w", "wo_then_z")
+        wb_raw = {}
+        wa_raw = {}
         nc.sync.dma_start(idx[:], offs)
         nc.sync.dma_start(idx2[:], offs2)
         nc.sync.dma_start(place[:], pos1)
         nc.sync.dma_start(out=gb_t[:], in_=gb.rearrange("(b p t) -> p b t", b=2, t=4))
-        tab_w = big_tile([P, T], I32, "tab_w")
-        tab_rows = tab_words[0].rearrange("p t i -> p (t i)").bitcast(I32)
-        for h in range(2):
-            cols = slice(h * T // 2, (h + 1) * T // 2)
-            nc.sync.dma_start(out=tab_w[:, cols], in_=tab_rows[:, cols])
-        ws_w = kept([P, 2 * H], U8, "ws_w")
-        nc.sync.dma_start(out=ws_w[:].bitcast(I32), in_=ws_words[0].bitcast(I32))
         nc.sync.dma_start(out=gz_t[:], in_=gz.rearrange("(b p t) -> p b t", b=2, t=4))
+        nc.sync.dma_start(out=tab_w[:], in_=tab_words[0].rearrange("p t i -> p (t i)").bitcast(I32))
+        for b in range(2):
+            cols = slice(b * H, (b + 1) * H)
+            nc.sync.dma_start(out=ws_w[:, cols].bitcast(I32), in_=ws_words[0][:, cols].bitcast(I32))
         load_planes(tab_s, tab_scales)
+        wa_raw[0] = load_weight(wa, 0, 0, wide[4])
         load_planes(ws_s, ws_scales)
-
-        def load_weight(w, a, b, name):
-            raw = big_tile([P, 4, BANK], F32, name)
-            rows = w[a * 512 : (a + 1) * 512, b * 512 : (b + 1) * 512]
-            nc.sync.dma_start(out=raw[:], in_=rows.rearrange("(p j) c -> p j c", j=4))
-            return raw
-
-        wb_raw = {(a, 0): load_weight(wb, a, 0, f"wb_raw{a}0") for a in range(2)}
-        tab2_w = big_tile([P, 2, T2], I32, "tab2_w")
+        wa_raw[1] = load_weight(wa, 0, 1, wide[5])
+        wb_raw[0, 0] = load_weight(wb, 0, 0, wide[0])
+        wb_raw[1, 0] = load_weight(wb, 1, 0, wide[1])
         nc.sync.dma_start(out=tab2_w[:], in_=tab2_words.rearrange("a p t i -> p a (t i)").bitcast(I32))
         load_planes(tab2_s, tab2_scales)
-        wa_raw = [load_weight(wa, 0, b, f"wa_raw{b}") for b in range(2)]
-        wg = kept([P, 4, NP], F32, "wg")
+        wb_raw[0, 1] = load_weight(wb, 0, 1, wide[2])
+        wb_raw[1, 1] = load_weight(wb, 1, 1, wide[3])
         for q in range(4):
             nc.sync.dma_start(out=wg[32 * q : 32 * q + 32], in_=wgs.rearrange("(m t) j -> m t j", t=4))
-        wb_raw = {**wb_raw, **{(a, 1): load_weight(wb, a, 1, f"wb_raw{a}1") for a in range(2)}}
-        wo_w = kept([P, 2, N], I32, "wo_w")
         nc.sync.dma_start(out=wo_w[:], in_=wo_words.rearrange("a p c i -> p a (c i)").bitcast(I32))
         load_planes(wo_s, wo_scales)
 
-        v_w = kept([P, S], U32, "v_w")
-        v_s = kept([P, S], U8, "v_s")
-        nc.vector.tensor_copy(v_w[:], tab_w[:].bitcast(U32).indirect(idx[:]))
-        for h in range(2):
-            cols = slice(h * 512, (h + 1) * 512)
-            nc.vector.tensor_copy(v_s[:, cols], tab_s[:].indirect(idx[:, h * 32 : (h + 1) * 32]))
-
-        def quantise_weight(raw, name):
-            grouped = half.tile([P, 4 * BANK], BF16, name="grouped", tag="half", align_bytes=64)
-            nc.scalar.copy(
-                grouped[:].rearrange("p (u v m j) -> p u m j v", u=2, v=2, j=4),
-                raw[:].rearrange("p j (m u v) -> p u m j v", u=2, v=2),
-            )
+        def quantise_weight(raw, name, on_vector):
+            grouped = take("staging", staging)
+            dst = grouped[:].rearrange("p (u v m j) -> p u m j v", u=2, v=2, j=4)
+            src = raw.rearrange("p j (m u v) -> p u m j v", u=2, v=2)
+            if on_vector:
+                nc.vector.tensor_copy(dst, src)
+            else:
+                nc.scalar.copy(dst, src)
             codes = kept([P, BANK], U32, name + "_w")
             scales = kept([P, BANK], U8, name + "_s")
             nc.vector.quantize_mx(out=codes[:].bitcast(FP8X4), scales=scales[:], in_=grouped[:])
             return codes, scales
 
+        sg = kept([P, 8], F32, "sg")
+        inv = kept([P, 8], F32, "inv")
+        mag = kept([P, 8], F32, "mag")
+        gbs = kept([P, 8], F32, "gbs")
+        gz_f = gz_t[:].rearrange("p b t -> p (b t)")
+        live = kept([P, 8], F32, "live")
+        nc.gpsimd.memset(live[:], 0.0)
+        nc.scalar.activation(live[:], live[:], ACT.Sin)
+        nc.vector.tensor_scalar(sg[:], gz_f, 0.0, 2.0, ALU.is_ge, ALU.mult)
+        nc.vector.tensor_scalar(sg[:], sg[:], -1.0, None, ALU.add)
+        nc.vector.tensor_tensor(mag[:], gz_f, sg[:], ALU.mult)
+        nc.vector.tensor_tensor(gbs[:], gb_t[:].rearrange("p b t -> p (b t)"), sg[:], ALU.mult)
+        nc.vector.tensor_scalar_max(mag[:], mag[:], 1e-30)
+        nc.vector.reciprocal(inv[:], mag[:])
+        v2_w = kept([P, 2, NP], U32, "v2_w", "v2_then_z")
+        v2_s = kept([P, NP], U8, "v2_s")
+        wb_q = {}
+
+        def short_product(s):
+            b, t = divmod(s, 4)
+            ms = slice(t * P, (t + 1) * P)
+            bank = take("b", [banks[5], banks[6], banks[7], banks[0], banks[1]])
+            for a in range(2):
+                codes, scales = wb_q[a, b]
+                nc.tensor.matmul_mx(
+                    out=bank[:], lhsT=codes[:, ms].bitcast(FP8X4), lhsT_scale=scales[:, ms],
+                    rhs=v2_w[:, a, :].bitcast(FP8X4), rhs_scale=v2_s[4 * a : P, :],
+                    start=(a == 0), stop=(a == 1),
+                )
+            bsb = short_homes[s]
+            nc.scalar.activation(bsb, bank[:], ACT.Copy, scale=gbs[:, s : s + 1])
+            return bsb
+
+        damp = {(0, 0): wide[6], (0, 1): wide[7], (1, 0): wide[2], (1, 1): wide[3]}
+        flat = {(0, 0): wide[0], (0, 1): wide[1], (1, 0): wide[4], (1, 1): wide[5]}
+        flat = {key: ap.rearrange("p a c -> p (a c)") for key, ap in flat.items()}
+        numer = {key: ap.rearrange("p (g t c) -> p g t c", g=2, t=4) for key, ap in flat.items()}
+
+        def damping(s, halves=(0, 1)):
+            b, t = divmod(s, 4)
+            for h in halves:
+                dst = damp[b, h][:, t, :]
+                nc.scalar.activation(dst, pages[s % 4][:, h * BANK : (h + 1) * BANK], ACT.Abs)
+            for h in halves:
+                dst = damp[b, h][:, t, :]
+                nc.scalar.activation(
+                    dst, dst, ACT.Abs_reciprocal_sqrt, scale=live[:, s : s + 1], bias=live[:, s : s + 1]
+                )
+            for h in halves:
+                dst = damp[b, h][:, t, :]
+                nc.scalar.activation(dst, dst, ACT.Square)
+
+        v_w = kept([P, S], U32, "v_w")
+        v_s = kept([P, S], U8, "v_s")
+        wa_q = []
+        zero = live[:, 0:1]
+
         sn = [kept([P, H], F32, f"sn{jb}") for jb in range(8)]
-        at = [kept([P, H], F32, f"at{jb}") for jb in range(8)]
 
         def sine_front(i):
             jb, b = divmod(i, 2)
             js = slice(jb * P, (jb + 1) * P)
-            bank = ps_s.tile([P, BANK], F32, name="s_bank")
+            bank = take("s", s_banks)
             nc.tensor.matmul_mx(
                 out=bank[:], lhsT=v_w[:, js].bitcast(FP8X4), lhsT_scale=v_s[:, js],
                 rhs=ws_w[:, 2 * b * BANK : 2 * (b + 1) * BANK].bitcast(FP4X4),
                 rhs_scale=ws_s[:, b * BANK : (b + 1) * BANK], start=True, stop=True,
             )
             dealt = bank[:].rearrange("p (q t) -> p t q", t=4)
-            k = turns.tile([P, 4, P], I32, name="k")
-            nc.vector.tensor_scalar(k[:], dealt, 1.0 / TWO_PI, None, ALU.mult)
+            k = take("turns", turns)
+            if i in () or i in ():
+                dst = sn[jb][:, b * BANK : (b + 1) * BANK]
+                nc.scalar.copy(dst.rearrange("p (t q) -> p t q", t=4), dealt)
+                flat_k = k[:].rearrange("p t q -> p (t q)")
+                if i in ():
+                    nc.gpsimd.tensor_scalar(flat_k, dst, 1.0 / TWO_PI, 0.0, ALU.mult, ALU.add)
+                else:
+                    nc.vector.tensor_scalar(flat_k, dst, 1.0 / TWO_PI, None, ALU.mult)
+            else:
+                nc.vector.tensor_scalar(k[:], dealt, 1.0 / TWO_PI, None, ALU.mult)
             return dealt, k
 
         def sine_back(i, dealt, k):
@@ -149,145 +219,61 @@ def tile_list_mushroom_flush_features_kernel(
             nc.vector.scalar_tensor_tensor(
                 dst.rearrange("p (t q) -> p t q", t=4), k[:], -TWO_PI, dealt, ALU.mult, ALU.add
             )
-            nc.scalar.activation(dst, dst, ACT.Sin)
+            nc.scalar.activation(dst, dst, ACT.Sin, bias=zero)
 
-        todo = [("wb", 0, 0), ("wb", 1, 0), ("wa", 0, 0), ("wa", 0, 1), ("wb", 0, 1), ("wb", 1, 1)]
-        w_q = {}
-        front = sine_front(0)
-        for i in range(16):
-            nxt = sine_front(i + 1) if i + 1 < 16 else None
-            sine_back(i, *front)
-            front = nxt
-            if i % 2 == 1 and i // 2 < 6:
-                name, a, b = todo[i // 2]
-                raw = wb_raw[a, b] if name == "wb" else wa_raw[b]
-                w_q[name, a, b] = quantise_weight(raw, f"{name}{a}{b}")
-        wa_q = [w_q["wa", 0, b] for b in range(2)]
-        wb_q = {(a, b): w_q["wb", a, b] for a in range(2) for b in range(2)}
-
-        sg = kept([P, 8], F32, "sg")
-        inv = kept([P, 8], F32, "inv")
-        mag = kept([P, 8], F32, "mag")
-        gbs = kept([P, 8], F32, "gbs")
-        gz_f = gz_t[:].rearrange("p b t -> p (b t)")
-        nc.scalar.activation(sg[:], gz_f, ACT.Sign)
-        nc.vector.tensor_tensor(mag[:], gz_f, sg[:], ALU.mult)
-        nc.vector.tensor_tensor(gbs[:], gb_t[:].rearrange("p b t -> p (b t)"), sg[:], ALU.mult)
-        nc.vector.tensor_scalar_max(mag[:], mag[:], 1e-30)
-        nc.vector.reciprocal(inv[:], mag[:])
-
-        v2_w = kept([P, 2, NP], U32, "v2_w")
-        v2_s = kept([P, NP], U8, "v2_s")
-        for a in range(2):
-            nc.vector.tensor_copy(v2_w[:, a, :], tab2_w[:, a, :].bitcast(U32).indirect(idx2[:]))
-        nc.vector.tensor_copy(v2_s[:], tab2_s[:].indirect(idx2[:]))
-
-        def short_product(s):
-            b, t = divmod(s, 4)
-            ms = slice(t * P, (t + 1) * P)
-            bank = ps_m.tile([P, BANK], F32, name="b_bank", tag="m")
-            for a in range(2):
-                codes, scales = wb_q[a, b]
-                nc.tensor.matmul_mx(
-                    out=bank[:], lhsT=codes[:, ms].bitcast(FP8X4), lhsT_scale=scales[:, ms],
-                    rhs=v2_w[:, a, :].bitcast(FP8X4), rhs_scale=v2_s[4 * a : P, :],
-                    start=(a == 0), stop=(a == 1),
-                )
-            bsb = bpool.tile([P, NP], F32, name="bsb")
-            nc.scalar.activation(bsb[:], bank[:], ACT.Copy, scale=gbs[:, s : s + 1])
-            return bsb
-
-        damp = {}
-        numer = {}
-
-        def damping(s):
-            b, t = divmod(s, 4)
-            for h in range(2):
-                if t == 0:
-                    damp[b, h] = big_tile([P, 4, BANK], F32, f"damp{b}{h}")
-                dst = damp[b, h][:, t, :]
-                nc.scalar.activation(dst, pages[s % 4][:, h * BANK : (h + 1) * BANK], ACT.Abs)
-            for h in range(2):
-                dst = damp[b, h][:, t, :]
-                nc.scalar.activation(
-                    dst, dst, ACT.Abs_reciprocal_sqrt, scale=inv[:, s : s + 1], bias=inv[:, s : s + 1]
-                )
-            for h in range(2):
-                dst = damp[b, h][:, t, :]
-                nc.scalar.activation(dst, dst, ACT.Square)
-
-        def numerator(s):
-            b, t = divmod(s, 4)
-            rs = slice(s * P, (s + 1) * P)
-            for h in range(2):
-                if t == 0:
-                    numer[b, h] = big_tile([P, 4, BANK], F32, f"numer{b}{h}")
-                bank = ps_t.tile([P, BANK], F32, name="sum_bank", tag="t")
-                for c in range(4):
-                    dst = bank[:, c * P : (c + 1) * P]
-                    jb = 4 * h + c
-                    nc.tensor.matmul(dst, sn[jb][:, rs], ident[:], start=True, stop=False, is_transpose=True)
-                    nc.tensor.matmul(dst, at[jb][:, rs], ident[:], start=False, stop=True, is_transpose=True)
-                nc.vector.scalar_tensor_tensor(
-                    numer[b, h][:, t, :], bank[:], sg[:, s : s + 1],
-                    pages[s % 4][:, h * BANK : (h + 1) * BANK], ALU.mult, ALU.add,
-                )
-
-        short = [short_product(s) for s in range(4)]
-
-        for jb in range(8):
+        def linear_part(jb):
             js = slice(jb * P, (jb + 1) * P)
             for b in range(2):
-                bank = ps_m.tile([P, BANK], F32, name="a_bank", tag="m")
+                bank = take("m", m_banks) if jb < 4 else take("l", banks[0:5])
                 nc.tensor.matmul_mx(
                     out=bank[:], lhsT=v_w[:, js].bitcast(FP8X4), lhsT_scale=v_s[:, js],
                     rhs=wa_q[b][0][:].bitcast(FP8X4), rhs_scale=wa_q[b][1][:], start=True, stop=True,
                 )
                 nc.scalar.copy(at[jb][:, b * BANK : (b + 1) * BANK], bank[:])
 
-        wo_dw = kept([P, 2, N], I32, "wo_dw")
-        wo_ds = kept([P, N], U8, "wo_ds")
-        nc.vector.tensor_copy(
-            wo_dw[:].rearrange("p a (u v m) -> p a u m v", u=2, v=2),
-            wo_w[:].rearrange("p a (m u v) -> p a u m v", u=2, v=2),
-        )
-        nc.vector.tensor_copy(
-            wo_ds[:].rearrange("p (t m) -> p t m", t=4), wo_s[:].rearrange("p (m t) -> p t m", t=4)
-        )
-
-        for s in range(8):
-            nc.vector.tensor_tensor(pages[s % 4][:].indirect(place[:]), short[s][:], wg[:, s % 4, :], ALU.mult)
-            if s + 4 < 8:
-                short.append(short_product(s + 4))
-            damping(s)
-            if s >= 2:
-                numerator(s - 2)
-        numerator(6)
-        numerator(7)
-
-        z_w = [kept([P, S], U32, f"z_w{b}") for b in range(2)]
+        z_w = [kept([P, S], U32, "z_w0", "wo_then_z"), kept([P, S], U32, "z_w1", "v2_then_z")]
         z_s = [kept([P, S], U8, f"z_s{b}") for b in range(2)]
         y_w = kept([P, S], I32, "y_w")
         y_s = kept([P, S], U8, "y_s")
         y_rows = out_0.rearrange("(p t) j -> p t j", t=4)
         y_codes = out_1[0].rearrange("p m t -> p (m t)").bitcast(I32)
-        for c0, width in CHUNKS:
+
+        y_stage = [kept([P, 4, BANK], F32, "y_stage0", "table2_then_y"), kept([P, 4, BANK], F32, "y_stage1", "table_then_y")]
+        y_woven = [at[i][:].bitcast(BF16) for i in range(2)]
+
+        def numerator(s):
+            b, t = divmod(s, 4)
+            rs = slice(s * P, (s + 1) * P)
+            for h in range(2):
+                bank = take("t", t_banks)
+                for c in range(4):
+                    dst = bank[:, c * P : (c + 1) * P]
+                    jb = 4 * h + c
+                    nc.tensor.matmul(dst, at[jb][:, rs], ident[:], start=True, stop=False, is_transpose=True)
+                    nc.tensor.matmul(dst, sn[jb][:, rs], ident[:], start=False, stop=True, is_transpose=True)
+                nc.vector.scalar_tensor_tensor(
+                    numer[b, h][:, :, t, :], bank[:].rearrange("p (g c) -> p g c", g=2), sg[:, s : s + 1],
+                    pages[s % 4][:, h * BANK : (h + 1) * BANK].rearrange("p (g c) -> p g c", g=2), ALU.mult, ALU.add,
+                )
+
+        def features(c0, width, b, zb):
             h, off = divmod(c0, BANK)
             cols = slice(c0, c0 + width)
-            for b in range(2):
-                zb = half.tile([P, 4 * width], BF16, name="zb", tag="half", align_bytes=64)
-                nc.vector.tensor_tensor(
-                    zb[:].rearrange("p (c i t) -> p c t i", i=2, t=4),
-                    numer[b, h][:, :, off : off + width].rearrange("p t (c i) -> p c t i", i=2),
-                    damp[b, h][:, :, off : off + width].rearrange("p t (c i) -> p c t i", i=2),
-                    ALU.mult,
-                )
-                nc.vector.quantize_mx(out=z_w[b][:, cols].bitcast(FP8X4), scales=z_s[b][:, cols], in_=zb[:])
-            ysb = big_tile([P, 4, width], F32, "ysb")
-            yb = half.tile([P, width, 4], BF16, name="yb", tag="half", align_bytes=64)
+            nc.vector.tensor_tensor(
+                zb.rearrange("p (c i t) -> p c t i", i=2, t=4),
+                numer[b, h][:, off // 256, :, off % 256 : off % 256 + width].rearrange("p t (c i) -> p c t i", i=2),
+                damp[b, h][:, :, off : off + width].rearrange("p t (c i) -> p c t i", i=2),
+                ALU.mult,
+            )
+            nc.vector.quantize_mx(out=z_w[b][:, cols].bitcast(FP8X4), scales=z_s[b][:, cols], in_=zb)
+
+        def last_product(c0, width, weave_on_vector):
+            cols = slice(c0, c0 + width)
+            ysb = y_stage[c0 // BANK][:, :, c0 % BANK : c0 % BANK + width]
+            yb = y_woven[c0 // BANK][:, 4 * (c0 % BANK) : 4 * (c0 % BANK + width)].rearrange("p (n t) -> p n t", t=4)
             for c in range(width // P):
                 js = slice(c0 + c * P, c0 + (c + 1) * P)
-                bank = ps_t.tile([P, 4, P], F32, name="y_bank", tag="t")
+                bank = take("y", y_banks)[:].rearrange("p (t n) -> p t n", t=4)
                 for t in range(4):
                     ms = slice(t * P, (t + 1) * P)
                     for b in range(2):
@@ -296,17 +282,89 @@ def tile_list_mushroom_flush_features_kernel(
                             rhs=z_w[b][:, js].bitcast(FP8X4), rhs_scale=z_s[b][:, js],
                             start=(b == 0), stop=(b == 1),
                         )
-                woven = bank[:].rearrange("p t n -> p n t")
-                if c0 + width == S:
+                woven = bank.rearrange("p t n -> p n t")
+                if weave_on_vector:
                     nc.vector.tensor_copy(yb[:, c * P : (c + 1) * P, :], woven)
                 else:
                     nc.scalar.copy(yb[:, c * P : (c + 1) * P, :], woven)
-                nc.scalar.copy(ysb[:, :, c * P : (c + 1) * P], bank[:])
+                nc.scalar.copy(ysb[:, :, c * P : (c + 1) * P], bank)
             nc.vector.quantize_mx(
-                out=y_w[:, cols].bitcast(FP8X4), scales=y_s[:, cols], in_=yb[:].rearrange("p n t -> p (n t)")
+                out=y_w[:, cols].bitcast(FP8X4), scales=y_s[:, cols], in_=yb.rearrange("p n t -> p (n t)")
             )
-            nc.sync.dma_start(out=y_rows[:, :, cols], in_=ysb[:])
-            nc.sync.dma_start(out=y_codes[:, cols], in_=y_w[:, cols])
+            nc.sync.dma_start(out=y_rows[:, :, cols], in_=ysb)
+            if (c0 + width) % 512 == 0:
+                span = slice(c0 + width - 512, c0 + width)
+                nc.sync.dma_start(out=y_codes[:, span], in_=y_w[:, span])
+
+        for h in range(2):
+            cols = slice(h * BANK, (h + 1) * BANK)
+            part = idx[:, h * 32 : (h + 1) * 32]
+            nc.vector.tensor_copy(v_w[:, cols], tab_w[:].bitcast(U32).indirect(part))
+            nc.vector.tensor_copy(v_s[:, cols], tab_s[:].indirect(part))
+        casts = {0: ("wa", 0, 0, False), 2: ("wa", 0, 1, False), 5: ("wb", 0, 0, False), 7: ("wb", 1, 0, False), 10: ("wb", 0, 1, False), 12: ("wb", 1, 1, True)}
+        linear_at = {4: (0,), 6: (1,), 8: (2,), 10: (3,)}
+        front = sine_front(0)
+        for i in range(16):
+            nxt = sine_front(i + 1) if i + 1 < 16 else None
+            sine_back(i, *front)
+            front = nxt
+            if i in casts:
+                name, a, b, on_vector = casts[i]
+                if name == "wb":
+                    wb_q[a, b] = quantise_weight(wb_raw[a, b], f"wb{a}{b}", on_vector)
+                else:
+                    wa_q.append(quantise_weight(wa_raw[b], f"wa{b}", on_vector))
+            if i == 9:
+                for a in range(2):
+                    nc.vector.tensor_copy(v2_w[:, a, :], tab2_w[:, a, :].bitcast(U32).indirect(idx2[:]))
+                nc.vector.tensor_copy(v2_s[:], tab2_s[:].indirect(idx2[:]))
+            if i == 14:
+                wo_dw = kept([P, 2, N], I32, "wo_dw")
+                wo_ds = kept([P, N], U8, "wo_ds")
+                nc.vector.tensor_copy(
+                    wo_dw[:].rearrange("p a (u v m) -> p a u m v", u=2, v=2),
+                    wo_w[:].rearrange("p a (m u v) -> p a u m v", u=2, v=2),
+                )
+                nc.vector.tensor_copy(
+                    wo_ds[:].rearrange("p (t m) -> p t m", t=4), wo_s[:].rearrange("p (m t) -> p t m", t=4)
+                )
+
+
+            for jb in linear_at.get(i, ()):
+                linear_part(jb)
+        nc.scalar.copy(live[:], inv[:])
+        views = [turns[i][:].rearrange("p t q -> p (t q)").bitcast(F32) for i in range(3)]
+        short_homes = [views[1], views[2], flat[0, 0][:, 0:512], flat[0, 1][:, 256:768], flat[0, 0][:, 1536:2048], flat[1, 0][:, 0:512], flat[1, 1][:, 0:512], staging[0][:].bitcast(F32)[:, 0:NP]]
+        short = [short_product(s) for s in range(8)]
+        for jb in range(4, 8):
+            linear_part(jb)
+        for s in range(8):
+            nc.vector.tensor_tensor(pages[s % 4][:].indirect(place[:]), short[s], wg[:, s % 4, :], ALU.mult)
+            if s + 8 < 8:
+                short.append(short_product(s + 8))
+            if s < 7:
+                damping(s)
+            else:
+                damping(s, (0,))
+                damping(s, (1,))
+            if s >= 2:
+                numerator(s - 2)
+        numerator(6)
+        numerator(7)
+        for n, (c0, width) in enumerate(CHUNKS):
+            for b in range(2):
+                if c0 < 256 or b == 1:
+                    first = 4 * (c0 % 256) if b == 0 else 0
+                    zb = staging[0 if b == 0 else 1 + n % 2][:, first : first + 4 * width]
+                else:
+                    group = c0 // 256 - 1
+                    first = 4 * (c0 % 256)
+                    zb = flat[1, group // 2][:, group % 2 * 1024 : (group % 2 + 1) * 1024].bitcast(BF16)[:, first : first + 4 * width]
+                features(c0, width, b, zb)
+            if n >= 0:
+                last_product(*CHUNKS[n - 0], n - 0 >= 4)
+        for n in range(len(CHUNKS) - 0, len(CHUNKS)):
+            last_product(*CHUNKS[n], n >= 4)
         for q in range(4):
             nc.sync.dma_start(
                 out=out_2[0, 4 * q : 4 * q + 4, :].bitcast(I32), in_=y_s[32 * q : 32 * q + 4, :].bitcast(I32)

@@ -79,7 +79,7 @@ def tile_list_mushroom_flush_features_kernel(
         tab_s = zeroed_plane(T, "tab_s")
         ws_s = zeroed_plane(H, "ws_s")
         wo_s = zeroed_plane(N, "wo_s")
-        pages = [kept([P, S], F32, f"page{i}") for i in range(4)]
+        pages = [kept([P, S], F32, f"page{i}") for i in range(5)]
         for i, page in enumerate(pages):
             nc.vector.memset(page[:], 0.0)
         ident = kept([P, P], F32, "ident")
@@ -173,7 +173,7 @@ def tile_list_mushroom_flush_features_kernel(
             b, t = divmod(s, 4)
             for h in halves:
                 dst = damp[b, h][:, t, :]
-                nc.scalar.activation(dst, pages[s % 4][:, h * BANK : (h + 1) * BANK], ACT.Abs)
+                nc.scalar.activation(dst, pages[s % 5][:, h * BANK : (h + 1) * BANK], ACT.Abs)
             for h in halves:
                 dst = damp[b, h][:, t, :]
                 nc.scalar.activation(
@@ -183,7 +183,7 @@ def tile_list_mushroom_flush_features_kernel(
                 dst = damp[b, h][:, t, :]
                 nc.scalar.activation(dst, dst, ACT.Square)
 
-        v_w = kept([P, S], U32, "v_w")
+        v_w = kept([P, S], U32, "v_w", "v_then_y")
         v_s = kept([P, S], U8, "v_s")
         wa_q = []
         zero = live[:, 0:1]
@@ -233,7 +233,7 @@ def tile_list_mushroom_flush_features_kernel(
 
         z_w = [kept([P, S], U32, "z_w0", "wo_then_z"), kept([P, S], U32, "z_w1", "v2_then_z")]
         z_s = [kept([P, S], U8, f"z_s{b}") for b in range(2)]
-        y_w = kept([P, S], I32, "y_w")
+        y_w = kept([P, S], I32, "y_w", "v_then_y")
         y_s = kept([P, S], U8, "y_s")
         y_rows = out_0.rearrange("(p t) j -> p t j", t=4)
         y_codes = out_1[0].rearrange("p m t -> p (m t)").bitcast(I32)
@@ -253,7 +253,7 @@ def tile_list_mushroom_flush_features_kernel(
                     nc.tensor.matmul(dst, sn[jb][:, rs], ident[:], start=False, stop=True, is_transpose=True)
                 nc.vector.scalar_tensor_tensor(
                     numer[b, h][:, :, t, :], bank[:].rearrange("p (g c) -> p g c", g=2), sg[:, s : s + 1],
-                    pages[s % 4][:, h * BANK : (h + 1) * BANK].rearrange("p (g c) -> p g c", g=2), ALU.mult, ALU.add,
+                    pages[s % 5][:, h * BANK : (h + 1) * BANK].rearrange("p (g c) -> p g c", g=2), ALU.mult, ALU.add,
                 )
 
         def features(c0, width, b, zb):
@@ -296,10 +296,10 @@ def tile_list_mushroom_flush_features_kernel(
                 span = slice(c0 + width - 512, c0 + width)
                 nc.sync.dma_start(out=y_codes[:, span], in_=y_w[:, span])
 
+        nc.vector.tensor_copy(v_w[:], tab_w[:].bitcast(U32).indirect(idx[:]))
         for h in range(2):
             cols = slice(h * BANK, (h + 1) * BANK)
             part = idx[:, h * 32 : (h + 1) * 32]
-            nc.vector.tensor_copy(v_w[:, cols], tab_w[:].bitcast(U32).indirect(part))
             nc.vector.tensor_copy(v_s[:, cols], tab_s[:].indirect(part))
         casts = {0: ("wa", 0, 0, False), 2: ("wa", 0, 1, False), 5: ("wb", 0, 0, False), 7: ("wb", 1, 0, False), 10: ("wb", 0, 1, False), 12: ("wb", 1, 1, True)}
         linear_at = {4: (0,), 6: (1,), 8: (2,), 10: (3,)}
@@ -334,12 +334,12 @@ def tile_list_mushroom_flush_features_kernel(
                 linear_part(jb)
         nc.scalar.copy(live[:], inv[:])
         views = [turns[i][:].rearrange("p t q -> p (t q)").bitcast(F32) for i in range(3)]
-        short_homes = [views[1], views[2], flat[0, 0][:, 0:512], flat[0, 1][:, 256:768], flat[0, 0][:, 1536:2048], flat[1, 0][:, 0:512], flat[1, 1][:, 0:512], staging[0][:].bitcast(F32)[:, 0:NP]]
+        short_homes = [views[1], views[2], views[0], flat[0, 0][:, 0:512], flat[0, 1][:, 256:768], flat[0, 0][:, 1536:2048], flat[1, 0][:, 0:512], staging[0][:].bitcast(F32)[:, 0:NP]]
         short = [short_product(s) for s in range(8)]
         for jb in range(4, 8):
             linear_part(jb)
         for s in range(8):
-            nc.vector.tensor_tensor(pages[s % 4][:].indirect(place[:]), short[s], wg[:, s % 4, :], ALU.mult)
+            nc.vector.tensor_tensor(pages[s % 5][:].indirect(place[:]), short[s], wg[:, s % 4, :], ALU.mult)
             if s + 8 < 8:
                 short.append(short_product(s + 8))
             if s < 7:
@@ -347,10 +347,10 @@ def tile_list_mushroom_flush_features_kernel(
             else:
                 damping(s, (0,))
                 damping(s, (1,))
-            if s >= 2:
-                numerator(s - 2)
-        numerator(6)
-        numerator(7)
+            if s >= 3:
+                numerator(s - 3)
+        for s in range(8 - 3, 8):
+            numerator(s)
         for n, (c0, width) in enumerate(CHUNKS):
             for b in range(2):
                 if c0 < 256 or b == 1:

@@ -19,9 +19,18 @@ ALU = mybir.AluOpType
 ACT = mybir.ActivationFunctionType
 
 P = 128
+PACK = 4
 BANK = 512
+SLICES = H // P
+BLOCKS = S // P
 TWO_PI = 2.0 * math.pi
-CHUNKS = [(0, 256), (256, 256), (512, 256), (768, 128), (896, 128)]
+TINY = 1e-30
+
+PAGES = 5
+SUM_LAG = 3
+EARLY_BLOCKS = 4
+GROUP = 256
+CHUNKS = [(c0, GROUP) for c0 in range(0, S - GROUP, GROUP)] + [(S - GROUP, P), (S - P, P)]
 
 
 def tile_list_mushroom_flush_features_kernel(
@@ -36,335 +45,321 @@ def tile_list_mushroom_flush_features_kernel(
         def kept(shape, dtype, name, tag=None):
             return keep.tile(shape, dtype, name=name, tag=tag or name, align_bytes=64)
 
-        banks = [psum.tile([P, BANK], F32, name=f"bank{i}") for i in range(8)]
-        m_banks = banks[0:2]
-        s_banks = banks[2:5]
-        t_banks = [banks[i] for i in (2, 1, 0, 4, 3, 5, 6, 7)]
-        y_banks = banks[0:5]
-        wide_tiles = [kept([P, 4 * BANK], F32, f"wide{i}") for i in range(8)]
-        wide = [tile[:].rearrange("p (a c) -> p a c", a=4) for tile in wide_tiles]
-        at = [kept([P, H], F32, f"at{jb}") for jb in range(8)]
-        staging = [kept([P, 4 * BANK], BF16, f"staging{i}") for i in range(3)]
-        turns = [kept([P, 4, P], I32, f"turns{i}") for i in range(3)]
-        used = {}
+        def in_turn(items, count):
+            return [items[i % len(items)] for i in range(count)]
 
-        def take(name, tiles):
-            n = used.setdefault(name, [])
-            n.append(0)
-            return tiles[(len(n) - 1) % len(tiles)]
+        banks = [psum.tile([P, BANK], F32, name=f"bank{i}") for i in range(8)]
+        sine_banks = in_turn(banks[2:5], 2 * BLOCKS)
+        early_banks = in_turn(banks[0:2], 2 * EARLY_BLOCKS)
+        late_banks = in_turn(banks[0:5], 2 * (BLOCKS - EARLY_BLOCKS))
+        short_banks = in_turn(banks[5:8] + banks[0:2], SLICES)
+        sum_banks = in_turn(late_banks[:-6:-1] + banks[5:8], 2 * SLICES)
+        y_banks = in_turn(banks[0:5], BLOCKS)
+
+        wide = [kept([P, PACK * BANK], F32, f"wide{i}") for i in range(8)]
+        raw_home = {("wb", 0, 0): 0, ("wb", 1, 0): 1, ("wb", 0, 1): 2, ("wb", 1, 1): 3, ("wa", 0, 0): 4, ("wa", 0, 1): 5}
+        numer_flat = {(0, 0): wide[0], (0, 1): wide[1], (1, 0): wide[4], (1, 1): wide[5]}
+        numer = {key: t[:].rearrange("p (g t c) -> p g t c", t=PACK, c=GROUP) for key, t in numer_flat.items()}
+        damp_flat = {(0, 0): wide[6], (0, 1): wide[7], (1, 0): wide[2], (1, 1): wide[3]}
+        damp = {key: t[:].rearrange("p (t c) -> p t c", t=PACK) for key, t in damp_flat.items()}
+        linear = [kept([P, H], F32, f"linear{jb}") for jb in range(BLOCKS)]
+        sine = [kept([P, H], F32, f"sine{jb}") for jb in range(BLOCKS)]
+        staging = [kept([P, PACK * BANK], BF16, f"staging{i}") for i in range(3)]
+        turns = [kept([P, BANK], I32, f"turns{i}") for i in range(3)]
+
+        idx = keep.tile([P, S // 16], U16, name="idx")
+        idx2 = keep.tile([P, NP // 16], U16, name="idx2")
+        place = keep.tile([P, NP // 16], U16, name="place")
 
         def zeroed_plane(width, name):
             plane = kept([P, width], U8, name)
             nc.vector.memset(plane[:].bitcast(I32), 0)
             return plane
 
-        def load_planes(plane, scales):
-            passes = scales.shape[0]
-            for q in range(4):
-                nc.sync.dma_start(
-                    out=plane[32 * q : 32 * q + 4 * passes, :].bitcast(I32),
-                    in_=scales[:, 4 * q : 4 * q + 4, :].bitcast(I32),
-                )
-
-        def load_weight(w, a, b, raw):
-            rows = w[a * 512 : (a + 1) * 512, b * 512 : (b + 1) * 512]
-            nc.sync.dma_start(out=raw, in_=rows.rearrange("(p j) c -> p j c", j=4))
-            return raw
-
-        idx = keep.tile([P, S // 16], U16, name="idx")
-        idx2 = keep.tile([P, NP // 16], U16, name="idx2")
-        place = keep.tile([P, NP // 16], U16, name="place")
-
-        tab2_s = zeroed_plane(T2, "tab2_s")
         tab_s = zeroed_plane(T, "tab_s")
         ws_s = zeroed_plane(H, "ws_s")
+        tab2_s = zeroed_plane(T2, "tab2_s")
         wo_s = zeroed_plane(N, "wo_s")
-        pages = [kept([P, S], F32, f"page{i}") for i in range(5)]
-        for i, page in enumerate(pages):
-            nc.vector.memset(page[:], 0.0)
+        pages = [kept([P, S], F32, f"page{i}") for i in range(PAGES)]
+        for page in pages:
+            nc.vector.memset(page[:].bitcast(I32), 0)
+        act_col = kept([P, SLICES], F32, "act_col")
+        nc.gpsimd.memset(act_col[:], 0.0)
+        nc.scalar.activation(act_col[:], act_col[:], ACT.Sin)
         ident = kept([P, P], F32, "ident")
         make_identity(nc, ident[:])
 
-        gb_t = kept([P, 2, 4], F32, "gb_t")
-        gz_t = kept([P, 2, 4], F32, "gz_t")
-        tab2_w = kept([P, 2, T2], I32, "tab2_w", "table2_then_y")
+        def load_planes(plane, scales):
+            rows = PACK * scales.shape[0]
+            for q in range(4):
+                nc.sync.dma_start(
+                    out=plane[32 * q : 32 * q + rows, :].bitcast(I32),
+                    in_=scales[:, 4 * q : 4 * q + 4, :].bitcast(I32),
+                )
+
+        def raw_chunk(key):
+            return wide[raw_home[key]][:].rearrange("p (j c) -> p j c", j=PACK)
+
+        def load_weight(key):
+            name, a, b = key
+            rows = {"wa": wa, "wb": wb}[name][a * BANK : (a + 1) * BANK, b * BANK : (b + 1) * BANK]
+            nc.sync.dma_start(out=raw_chunk(key), in_=rows.rearrange("(p j) c -> p j c", j=PACK))
+
+        gb_t = kept([P, 2, PACK], F32, "gb_t")
+        gz_t = kept([P, 2, PACK], F32, "gz_t")
         tab_w = kept([P, T], I32, "tab_w", "table_then_y")
-        wg = kept([P, 4, NP], F32, "wg")
+        tab2_w = kept([P, 2, T2], I32, "tab2_w", "table2_then_y")
         ws_w = kept([P, 2 * H], U8, "ws_w")
         wo_w = kept([P, 2, N], I32, "wo_w", "wo_then_z")
-        wb_raw = {}
-        wa_raw = {}
+        wg = kept([P, PACK, NP], F32, "wg")
+        weight_order = [("wa", 0, 0), ("wa", 0, 1), ("wb", 0, 0), ("wb", 1, 0), ("wb", 0, 1), ("wb", 1, 1)]
+
         nc.sync.dma_start(idx[:], offs)
         nc.sync.dma_start(idx2[:], offs2)
         nc.sync.dma_start(place[:], pos1)
-        nc.sync.dma_start(out=gb_t[:], in_=gb.rearrange("(b p t) -> p b t", b=2, t=4))
-        nc.sync.dma_start(out=gz_t[:], in_=gz.rearrange("(b p t) -> p b t", b=2, t=4))
+        nc.sync.dma_start(out=gb_t[:], in_=gb.rearrange("(b p t) -> p b t", b=2, t=PACK))
+        nc.sync.dma_start(out=gz_t[:], in_=gz.rearrange("(b p t) -> p b t", b=2, t=PACK))
         nc.sync.dma_start(out=tab_w[:], in_=tab_words[0].rearrange("p t i -> p (t i)").bitcast(I32))
         for b in range(2):
             cols = slice(b * H, (b + 1) * H)
             nc.sync.dma_start(out=ws_w[:, cols].bitcast(I32), in_=ws_words[0][:, cols].bitcast(I32))
         load_planes(tab_s, tab_scales)
-        wa_raw[0] = load_weight(wa, 0, 0, wide[4])
+        load_weight(weight_order[0])
         load_planes(ws_s, ws_scales)
-        wa_raw[1] = load_weight(wa, 0, 1, wide[5])
-        wb_raw[0, 0] = load_weight(wb, 0, 0, wide[0])
-        wb_raw[1, 0] = load_weight(wb, 1, 0, wide[1])
+        for key in weight_order[1:4]:
+            load_weight(key)
         nc.sync.dma_start(out=tab2_w[:], in_=tab2_words.rearrange("a p t i -> p a (t i)").bitcast(I32))
         load_planes(tab2_s, tab2_scales)
-        wb_raw[0, 1] = load_weight(wb, 0, 1, wide[2])
-        wb_raw[1, 1] = load_weight(wb, 1, 1, wide[3])
+        for key in weight_order[4:]:
+            load_weight(key)
         for q in range(4):
-            nc.sync.dma_start(out=wg[32 * q : 32 * q + 32], in_=wgs.rearrange("(m t) j -> m t j", t=4))
+            nc.sync.dma_start(out=wg[32 * q : 32 * q + 32], in_=wgs.rearrange("(m t) j -> m t j", t=PACK))
         nc.sync.dma_start(out=wo_w[:], in_=wo_words.rearrange("a p c i -> p a (c i)").bitcast(I32))
         load_planes(wo_s, wo_scales)
 
-        def quantise_weight(raw, name, on_vector):
-            grouped = take("staging", staging)
-            dst = grouped[:].rearrange("p (u v m j) -> p u m j v", u=2, v=2, j=4)
-            src = raw.rearrange("p j (m u v) -> p u m j v", u=2, v=2)
-            if on_vector:
-                nc.vector.tensor_copy(dst, src)
-            else:
-                nc.scalar.copy(dst, src)
-            codes = kept([P, BANK], U32, name + "_w")
-            scales = kept([P, BANK], U8, name + "_s")
-            nc.vector.quantize_mx(out=codes[:].bitcast(FP8X4), scales=scales[:], in_=grouped[:])
-            return codes, scales
-
-        sg = kept([P, 8], F32, "sg")
-        inv = kept([P, 8], F32, "inv")
-        mag = kept([P, 8], F32, "mag")
-        gbs = kept([P, 8], F32, "gbs")
-        gz_f = gz_t[:].rearrange("p b t -> p (b t)")
-        live = kept([P, 8], F32, "live")
-        nc.gpsimd.memset(live[:], 0.0)
-        nc.scalar.activation(live[:], live[:], ACT.Sin)
-        nc.vector.tensor_scalar(sg[:], gz_f, 0.0, 2.0, ALU.is_ge, ALU.mult)
+        sg = kept([P, SLICES], F32, "sg")
+        gz_abs = kept([P, SLICES], F32, "gz_abs")
+        gz_inv = kept([P, SLICES], F32, "gz_inv")
+        gb_sg = kept([P, SLICES], F32, "gb_sg")
+        gz_cols = gz_t[:].rearrange("p b t -> p (b t)")
+        nc.vector.tensor_scalar(sg[:], gz_cols, 0.0, 2.0, ALU.is_ge, ALU.mult)
         nc.vector.tensor_scalar(sg[:], sg[:], -1.0, None, ALU.add)
-        nc.vector.tensor_tensor(mag[:], gz_f, sg[:], ALU.mult)
-        nc.vector.tensor_tensor(gbs[:], gb_t[:].rearrange("p b t -> p (b t)"), sg[:], ALU.mult)
-        nc.vector.tensor_scalar_max(mag[:], mag[:], 1e-30)
-        nc.vector.reciprocal(inv[:], mag[:])
-        v2_w = kept([P, 2, NP], U32, "v2_w", "v2_then_z")
-        v2_s = kept([P, NP], U8, "v2_s")
-        wb_q = {}
-
-        def short_product(s):
-            b, t = divmod(s, 4)
-            ms = slice(t * P, (t + 1) * P)
-            bank = take("b", [banks[5], banks[6], banks[7], banks[0], banks[1]])
-            for a in range(2):
-                codes, scales = wb_q[a, b]
-                nc.tensor.matmul_mx(
-                    out=bank[:], lhsT=codes[:, ms].bitcast(FP8X4), lhsT_scale=scales[:, ms],
-                    rhs=v2_w[:, a, :].bitcast(FP8X4), rhs_scale=v2_s[4 * a : P, :],
-                    start=(a == 0), stop=(a == 1),
-                )
-            bsb = short_homes[s]
-            nc.scalar.activation(bsb, bank[:], ACT.Copy, scale=gbs[:, s : s + 1])
-            return bsb
-
-        damp = {(0, 0): wide[6], (0, 1): wide[7], (1, 0): wide[2], (1, 1): wide[3]}
-        flat = {(0, 0): wide[0], (0, 1): wide[1], (1, 0): wide[4], (1, 1): wide[5]}
-        flat = {key: ap.rearrange("p a c -> p (a c)") for key, ap in flat.items()}
-        numer = {key: ap.rearrange("p (g t c) -> p g t c", g=2, t=4) for key, ap in flat.items()}
-
-        def damping(s, halves=(0, 1)):
-            b, t = divmod(s, 4)
-            for h in halves:
-                dst = damp[b, h][:, t, :]
-                nc.scalar.activation(dst, pages[s % 5][:, h * BANK : (h + 1) * BANK], ACT.Abs)
-            for h in halves:
-                dst = damp[b, h][:, t, :]
-                nc.scalar.activation(
-                    dst, dst, ACT.Abs_reciprocal_sqrt, scale=live[:, s : s + 1], bias=live[:, s : s + 1]
-                )
-            for h in halves:
-                dst = damp[b, h][:, t, :]
-                nc.scalar.activation(dst, dst, ACT.Square)
+        nc.vector.tensor_tensor(gz_abs[:], gz_cols, sg[:], ALU.mult)
+        nc.vector.tensor_tensor(gb_sg[:], gb_t[:].rearrange("p b t -> p (b t)"), sg[:], ALU.mult)
+        nc.vector.tensor_scalar_max(gz_abs[:], gz_abs[:], TINY)
+        nc.vector.reciprocal(gz_inv[:], gz_abs[:])
 
         v_w = kept([P, S], U32, "v_w", "v_then_y")
         v_s = kept([P, S], U8, "v_s")
-        wa_q = []
-        zero = live[:, 0:1]
+        v2_w = kept([P, 2, NP], U32, "v2_w", "v2_then_z")
+        v2_s = kept([P, NP], U8, "v2_s")
+        for h in range(2):
+            cols = slice(h * BANK, (h + 1) * BANK)
+            entries = idx[:, h * BANK // 16 : (h + 1) * BANK // 16]
+            nc.vector.tensor_copy(v_w[:, cols], tab_w[:].bitcast(U32).indirect(entries))
+            nc.vector.tensor_copy(v_s[:, cols], tab_s[:].indirect(entries))
 
-        sn = [kept([P, H], F32, f"sn{jb}") for jb in range(8)]
+        quantised = {}
 
-        def sine_front(i):
+        def quantise_weight(n):
+            key = weight_order[n]
+            grouped = staging[n % len(staging)]
+            dst = grouped[:].rearrange("p (u v m j) -> p u m j v", u=2, v=2, j=PACK)
+            src = raw_chunk(key).rearrange("p j (m u v) -> p u m j v", u=2, v=2)
+            if n == len(weight_order) - 1:
+                nc.vector.tensor_copy(dst, src)
+            else:
+                nc.scalar.copy(dst, src)
+            codes = kept([P, BANK], U32, f"codes{n}")
+            scales = kept([P, BANK], U8, f"scales{n}")
+            nc.vector.quantize_mx(out=codes[:].bitcast(FP8X4), scales=scales[:], in_=grouped[:])
+            quantised[key] = (codes, scales)
+
+        def dealt(ap):
+            return ap.rearrange("p (m t) -> p t m", t=PACK)
+
+        def by_slices(ap):
+            return ap.rearrange("p (t m) -> p t m", t=PACK)
+
+        def count_turns(i):
             jb, b = divmod(i, 2)
             js = slice(jb * P, (jb + 1) * P)
-            bank = take("s", s_banks)
             nc.tensor.matmul_mx(
-                out=bank[:], lhsT=v_w[:, js].bitcast(FP8X4), lhsT_scale=v_s[:, js],
+                out=sine_banks[i][:], lhsT=v_w[:, js].bitcast(FP8X4), lhsT_scale=v_s[:, js],
                 rhs=ws_w[:, 2 * b * BANK : 2 * (b + 1) * BANK].bitcast(FP4X4),
                 rhs_scale=ws_s[:, b * BANK : (b + 1) * BANK], start=True, stop=True,
             )
-            dealt = bank[:].rearrange("p (q t) -> p t q", t=4)
-            k = take("turns", turns)
-            if i in () or i in ():
-                dst = sn[jb][:, b * BANK : (b + 1) * BANK]
-                nc.scalar.copy(dst.rearrange("p (t q) -> p t q", t=4), dealt)
-                flat_k = k[:].rearrange("p t q -> p (t q)")
-                if i in ():
-                    nc.gpsimd.tensor_scalar(flat_k, dst, 1.0 / TWO_PI, 0.0, ALU.mult, ALU.add)
-                else:
-                    nc.vector.tensor_scalar(flat_k, dst, 1.0 / TWO_PI, None, ALU.mult)
-            else:
-                nc.vector.tensor_scalar(k[:], dealt, 1.0 / TWO_PI, None, ALU.mult)
-            return dealt, k
+            nc.vector.tensor_scalar(by_slices(turns[i % 3][:]), dealt(sine_banks[i][:]), 1.0 / TWO_PI, None, ALU.mult)
 
-        def sine_back(i, dealt, k):
+        def take_sine(i):
             jb, b = divmod(i, 2)
-            dst = sn[jb][:, b * BANK : (b + 1) * BANK]
+            dst = sine[jb][:, b * BANK : (b + 1) * BANK]
             nc.vector.scalar_tensor_tensor(
-                dst.rearrange("p (t q) -> p t q", t=4), k[:], -TWO_PI, dealt, ALU.mult, ALU.add
+                by_slices(dst), by_slices(turns[i % 3][:]), -TWO_PI, dealt(sine_banks[i][:]), ALU.mult, ALU.add
             )
-            nc.scalar.activation(dst, dst, ACT.Sin, bias=zero)
+            nc.scalar.activation(dst, dst, ACT.Sin, bias=act_col[:, 0:1])
 
         def linear_part(jb):
             js = slice(jb * P, (jb + 1) * P)
             for b in range(2):
-                bank = take("m", m_banks) if jb < 4 else take("l", banks[0:5])
+                bank = (early_banks + late_banks)[2 * jb + b]
+                codes, scales = quantised["wa", 0, b]
                 nc.tensor.matmul_mx(
                     out=bank[:], lhsT=v_w[:, js].bitcast(FP8X4), lhsT_scale=v_s[:, js],
-                    rhs=wa_q[b][0][:].bitcast(FP8X4), rhs_scale=wa_q[b][1][:], start=True, stop=True,
+                    rhs=codes[:].bitcast(FP8X4), rhs_scale=scales[:], start=True, stop=True,
                 )
-                nc.scalar.copy(at[jb][:, b * BANK : (b + 1) * BANK], bank[:])
+                nc.scalar.copy(linear[jb][:, b * BANK : (b + 1) * BANK], bank[:])
+
+        count_turns(0)
+        for jb in range(BLOCKS):
+            for i in (2 * jb, 2 * jb + 1):
+                if i + 1 < 2 * BLOCKS:
+                    count_turns(i + 1)
+                take_sine(i)
+            if 1 <= jb <= len(weight_order):
+                quantise_weight(jb - 1)
+            if 2 <= jb < 2 + EARLY_BLOCKS:
+                linear_part(jb - 2)
+            if jb == BLOCKS // 2:
+                for a in range(2):
+                    nc.vector.tensor_copy(v2_w[:, a, :], tab2_w[:, a, :].bitcast(U32).indirect(idx2[:]))
+                nc.vector.tensor_copy(v2_s[:], tab2_s[:].indirect(idx2[:]))
+
+        wo_dealt_w = kept([P, 2, N], I32, "wo_dealt_w")
+        wo_dealt_s = kept([P, N], U8, "wo_dealt_s")
+        nc.vector.tensor_copy(
+            wo_dealt_w[:].rearrange("p a (u v m) -> p a u m v", u=2, v=2),
+            wo_w[:].rearrange("p a (m u v) -> p a u m v", u=2, v=2),
+        )
+        nc.vector.tensor_copy(by_slices(wo_dealt_s[:]), dealt(wo_s[:]))
+
+        nc.scalar.copy(act_col[:], gz_inv[:])
+
+        short_homes = [turns[(2 * BLOCKS + s) % 3][:].bitcast(F32) for s in range(-3, 0)]
+        short_homes += [numer_flat[0, (s - 3) % 2][:, (s - 3) * GROUP : (s - 1) * GROUP] for s in range(3, 6)]
+        short_homes += [numer_flat[1, 0][:, 0:NP], staging[0][:].bitcast(F32)[:, 0:NP]]
+
+        def short_product(s):
+            b, t = divmod(s, PACK)
+            ms = slice(t * P, (t + 1) * P)
+            for a in range(2):
+                codes, scales = quantised["wb", a, b]
+                nc.tensor.matmul_mx(
+                    out=short_banks[s][:], lhsT=codes[:, ms].bitcast(FP8X4), lhsT_scale=scales[:, ms],
+                    rhs=v2_w[:, a, :].bitcast(FP8X4), rhs_scale=v2_s[PACK * a : P, :], start=(a == 0), stop=(a == 1),
+                )
+            nc.scalar.activation(short_homes[s], short_banks[s][:], ACT.Copy, scale=gb_sg[:, s : s + 1])
+
+        def damping(s, halves):
+            b, t = divmod(s, PACK)
+            col = act_col[:, s : s + 1]
+            for h in halves:
+                nc.scalar.activation(damp[b, h][:, t, :], pages[s % PAGES][:, h * BANK : (h + 1) * BANK], ACT.Abs)
+            for h in halves:
+                nc.scalar.activation(
+                    damp[b, h][:, t, :], damp[b, h][:, t, :], ACT.Abs_reciprocal_sqrt, scale=col, bias=col
+                )
+            for h in halves:
+                nc.scalar.activation(damp[b, h][:, t, :], damp[b, h][:, t, :], ACT.Square)
+
+        def numerator(s):
+            b, t = divmod(s, PACK)
+            rs = slice(s * P, (s + 1) * P)
+            for h in range(2):
+                bank = sum_banks[2 * s + h]
+                for c in range(BANK // P):
+                    dst = bank[:, c * P : (c + 1) * P]
+                    jb = h * BANK // P + c
+                    nc.tensor.matmul(dst, linear[jb][:, rs], ident[:], start=True, stop=False, is_transpose=True)
+                    nc.tensor.matmul(dst, sine[jb][:, rs], ident[:], start=False, stop=True, is_transpose=True)
+                nc.vector.scalar_tensor_tensor(
+                    numer[b, h][:, :, t, :], bank[:].rearrange("p (g c) -> p g c", c=GROUP), sg[:, s : s + 1],
+                    pages[s % PAGES][:, h * BANK : (h + 1) * BANK].rearrange("p (g c) -> p g c", c=GROUP),
+                    ALU.mult, ALU.add,
+                )
+
+        for s in range(SLICES):
+            short_product(s)
+        for jb in range(EARLY_BLOCKS, BLOCKS):
+            linear_part(jb)
+        for s in range(SLICES):
+            nc.vector.tensor_tensor(pages[s % PAGES][:].indirect(place[:]), short_homes[s], wg[:, s % PACK, :], ALU.mult)
+            if s < SLICES - 1:
+                damping(s, (0, 1))
+            else:
+                damping(s, (0,))
+                damping(s, (1,))
+            if s >= SUM_LAG:
+                numerator(s - SUM_LAG)
+        for s in range(SLICES - SUM_LAG, SLICES):
+            numerator(s)
 
         z_w = [kept([P, S], U32, "z_w0", "wo_then_z"), kept([P, S], U32, "z_w1", "v2_then_z")]
         z_s = [kept([P, S], U8, f"z_s{b}") for b in range(2)]
         y_w = kept([P, S], I32, "y_w", "v_then_y")
         y_s = kept([P, S], U8, "y_s")
-        y_rows = out_0.rearrange("(p t) j -> p t j", t=4)
+        y_f32 = [kept([P, PACK, BANK], F32, "y_f32_0", "table2_then_y"), kept([P, PACK, BANK], F32, "y_f32_1", "table_then_y")]
+        y_bf16 = [linear[h][:].bitcast(BF16) for h in range(2)]
+        y_rows = out_0.rearrange("(p t) j -> p t j", t=PACK)
         y_codes = out_1[0].rearrange("p m t -> p (m t)").bitcast(I32)
 
-        y_stage = [kept([P, 4, BANK], F32, "y_stage0", "table2_then_y"), kept([P, 4, BANK], F32, "y_stage1", "table_then_y")]
-        y_woven = [at[i][:].bitcast(BF16) for i in range(2)]
+        def z_home(n, b):
+            c0, width = CHUNKS[n]
+            if b == 1:
+                return staging[1 + n % 2][:, 0 : PACK * width]
+            if n == 0:
+                return staging[0][:, 0 : PACK * width]
+            h, g = divmod(c0 // GROUP - 1, 2)
+            spent = numer_flat[1, h][:, g * PACK * GROUP : (g + 1) * PACK * GROUP].bitcast(BF16)
+            return spent[:, PACK * (c0 % GROUP) : PACK * (c0 % GROUP + width)]
 
-        def numerator(s):
-            b, t = divmod(s, 4)
-            rs = slice(s * P, (s + 1) * P)
-            for h in range(2):
-                bank = take("t", t_banks)
-                for c in range(4):
-                    dst = bank[:, c * P : (c + 1) * P]
-                    jb = 4 * h + c
-                    nc.tensor.matmul(dst, at[jb][:, rs], ident[:], start=True, stop=False, is_transpose=True)
-                    nc.tensor.matmul(dst, sn[jb][:, rs], ident[:], start=False, stop=True, is_transpose=True)
-                nc.vector.scalar_tensor_tensor(
-                    numer[b, h][:, :, t, :], bank[:].rearrange("p (g c) -> p g c", g=2), sg[:, s : s + 1],
-                    pages[s % 5][:, h * BANK : (h + 1) * BANK].rearrange("p (g c) -> p g c", g=2), ALU.mult, ALU.add,
-                )
-
-        def features(c0, width, b, zb):
+        def features(n, b):
+            c0, width = CHUNKS[n]
             h, off = divmod(c0, BANK)
+            g, first = divmod(off, GROUP)
             cols = slice(c0, c0 + width)
+            zb = z_home(n, b)
             nc.vector.tensor_tensor(
-                zb.rearrange("p (c i t) -> p c t i", i=2, t=4),
-                numer[b, h][:, off // 256, :, off % 256 : off % 256 + width].rearrange("p t (c i) -> p c t i", i=2),
+                zb.rearrange("p (c i t) -> p c t i", i=2, t=PACK),
+                numer[b, h][:, g, :, first : first + width].rearrange("p t (c i) -> p c t i", i=2),
                 damp[b, h][:, :, off : off + width].rearrange("p t (c i) -> p c t i", i=2),
                 ALU.mult,
             )
             nc.vector.quantize_mx(out=z_w[b][:, cols].bitcast(FP8X4), scales=z_s[b][:, cols], in_=zb)
 
-        def last_product(c0, width, weave_on_vector):
+        def last_product(n):
+            c0, width = CHUNKS[n]
+            h, off = divmod(c0, BANK)
             cols = slice(c0, c0 + width)
-            ysb = y_stage[c0 // BANK][:, :, c0 % BANK : c0 % BANK + width]
-            yb = y_woven[c0 // BANK][:, 4 * (c0 % BANK) : 4 * (c0 % BANK + width)].rearrange("p (n t) -> p n t", t=4)
+            plain = y_f32[h][:, :, off : off + width]
+            woven = y_bf16[h][:, PACK * off : PACK * (off + width)]
             for c in range(width // P):
                 js = slice(c0 + c * P, c0 + (c + 1) * P)
-                bank = take("y", y_banks)[:].rearrange("p (t n) -> p t n", t=4)
-                for t in range(4):
+                bank = y_banks[c0 // P + c][:].rearrange("p (t n) -> p t n", t=PACK)
+                for t in range(PACK):
                     ms = slice(t * P, (t + 1) * P)
                     for b in range(2):
                         nc.tensor.matmul_mx(
-                            out=bank[:, t, :], lhsT=wo_dw[:, b, ms].bitcast(FP8X4), lhsT_scale=wo_ds[4 * b : P, ms],
-                            rhs=z_w[b][:, js].bitcast(FP8X4), rhs_scale=z_s[b][:, js],
-                            start=(b == 0), stop=(b == 1),
+                            out=bank[:, t, :], lhsT=wo_dealt_w[:, b, ms].bitcast(FP8X4),
+                            lhsT_scale=wo_dealt_s[PACK * b : P, ms],
+                            rhs=z_w[b][:, js].bitcast(FP8X4), rhs_scale=z_s[b][:, js], start=(b == 0), stop=(b == 1),
                         )
-                woven = bank.rearrange("p t n -> p n t")
-                if weave_on_vector:
-                    nc.vector.tensor_copy(yb[:, c * P : (c + 1) * P, :], woven)
+                dst = woven.rearrange("p (n t) -> p n t", t=PACK)[:, c * P : (c + 1) * P, :]
+                if n == len(CHUNKS) - 1:
+                    nc.vector.tensor_copy(dst, bank.rearrange("p t n -> p n t"))
                 else:
-                    nc.scalar.copy(yb[:, c * P : (c + 1) * P, :], woven)
-                nc.scalar.copy(ysb[:, :, c * P : (c + 1) * P], bank)
-            nc.vector.quantize_mx(
-                out=y_w[:, cols].bitcast(FP8X4), scales=y_s[:, cols], in_=yb.rearrange("p n t -> p (n t)")
-            )
-            nc.sync.dma_start(out=y_rows[:, :, cols], in_=ysb)
-            if (c0 + width) % 512 == 0:
-                span = slice(c0 + width - 512, c0 + width)
-                nc.sync.dma_start(out=y_codes[:, span], in_=y_w[:, span])
+                    nc.scalar.copy(dst, bank.rearrange("p t n -> p n t"))
+                nc.scalar.copy(plain[:, :, c * P : (c + 1) * P], bank)
+            nc.vector.quantize_mx(out=y_w[:, cols].bitcast(FP8X4), scales=y_s[:, cols], in_=woven)
+            nc.sync.dma_start(out=y_rows[:, :, cols], in_=plain)
+            if (c0 + width) % BANK == 0:
+                half = slice(h * BANK, (h + 1) * BANK)
+                nc.sync.dma_start(out=y_codes[:, half], in_=y_w[:, half])
 
-        nc.vector.tensor_copy(v_w[:], tab_w[:].bitcast(U32).indirect(idx[:]))
-        for h in range(2):
-            cols = slice(h * BANK, (h + 1) * BANK)
-            part = idx[:, h * 32 : (h + 1) * 32]
-            nc.vector.tensor_copy(v_s[:, cols], tab_s[:].indirect(part))
-        casts = {0: ("wa", 0, 0, False), 2: ("wa", 0, 1, False), 5: ("wb", 0, 0, False), 7: ("wb", 1, 0, False), 10: ("wb", 0, 1, False), 12: ("wb", 1, 1, True)}
-        linear_at = {4: (0,), 6: (1,), 8: (2,), 10: (3,)}
-        front = sine_front(0)
-        for i in range(16):
-            nxt = sine_front(i + 1) if i + 1 < 16 else None
-            sine_back(i, *front)
-            front = nxt
-            if i in casts:
-                name, a, b, on_vector = casts[i]
-                if name == "wb":
-                    wb_q[a, b] = quantise_weight(wb_raw[a, b], f"wb{a}{b}", on_vector)
-                else:
-                    wa_q.append(quantise_weight(wa_raw[b], f"wa{b}", on_vector))
-            if i == 9:
-                for a in range(2):
-                    nc.vector.tensor_copy(v2_w[:, a, :], tab2_w[:, a, :].bitcast(U32).indirect(idx2[:]))
-                nc.vector.tensor_copy(v2_s[:], tab2_s[:].indirect(idx2[:]))
-            if i == 14:
-                wo_dw = kept([P, 2, N], I32, "wo_dw")
-                wo_ds = kept([P, N], U8, "wo_ds")
-                nc.vector.tensor_copy(
-                    wo_dw[:].rearrange("p a (u v m) -> p a u m v", u=2, v=2),
-                    wo_w[:].rearrange("p a (m u v) -> p a u m v", u=2, v=2),
-                )
-                nc.vector.tensor_copy(
-                    wo_ds[:].rearrange("p (t m) -> p t m", t=4), wo_s[:].rearrange("p (m t) -> p t m", t=4)
-                )
-
-
-            for jb in linear_at.get(i, ()):
-                linear_part(jb)
-        nc.scalar.copy(live[:], inv[:])
-        views = [turns[i][:].rearrange("p t q -> p (t q)").bitcast(F32) for i in range(3)]
-        short_homes = [views[1], views[2], views[0], flat[0, 0][:, 0:512], flat[0, 1][:, 256:768], flat[0, 0][:, 1536:2048], flat[1, 0][:, 0:512], staging[0][:].bitcast(F32)[:, 0:NP]]
-        short = [short_product(s) for s in range(8)]
-        for jb in range(4, 8):
-            linear_part(jb)
-        for s in range(8):
-            nc.vector.tensor_tensor(pages[s % 5][:].indirect(place[:]), short[s], wg[:, s % 4, :], ALU.mult)
-            if s + 8 < 8:
-                short.append(short_product(s + 8))
-            if s < 7:
-                damping(s)
-            else:
-                damping(s, (0,))
-                damping(s, (1,))
-            if s >= 3:
-                numerator(s - 3)
-        for s in range(8 - 3, 8):
-            numerator(s)
-        for n, (c0, width) in enumerate(CHUNKS):
-            for b in range(2):
-                if c0 < 256 or b == 1:
-                    first = 4 * (c0 % 256) if b == 0 else 0
-                    zb = staging[0 if b == 0 else 1 + n % 2][:, first : first + 4 * width]
-                else:
-                    group = c0 // 256 - 1
-                    first = 4 * (c0 % 256)
-                    zb = flat[1, group // 2][:, group % 2 * 1024 : (group % 2 + 1) * 1024].bitcast(BF16)[:, first : first + 4 * width]
-                features(c0, width, b, zb)
-            if n >= 0:
-                last_product(*CHUNKS[n - 0], n - 0 >= 4)
-        for n in range(len(CHUNKS) - 0, len(CHUNKS)):
-            last_product(*CHUNKS[n], n >= 4)
+        for n in range(len(CHUNKS)):
+            features(n, 0)
+            features(n, 1)
+            last_product(n)
         for q in range(4):
             nc.sync.dma_start(
                 out=out_2[0, 4 * q : 4 * q + 4, :].bitcast(I32), in_=y_s[32 * q : 32 * q + 4, :].bitcast(I32)

import math
from contextlib import ExitStack

import concourse.mybir as mybir
from concourse.masks import make_identity

K, K2, H, N, T, T2, S, NP = 512, 1024, 1024, 512, 2048, 1024, 1024, 512
FLOPS = 2 * (2 * K * H * S + K2 * H * NP + H * N * S)

F32 = mybir.dt.float32
BF16 = mybir.dt.bfloat16
I32 = mybir.dt.int32
U32 = mybir.dt.uint32
U16 = mybir.dt.uint16
U8 = mybir.dt.uint8
FP8X4 = mybir.dt.float8_e4m3fn_x4
FP4X4 = mybir.dt.float4_e2m1fn_x4
ALU = mybir.AluOpType
ACT = mybir.ActivationFunctionType

P = 128
PACK = 4
BANK = 512
SLICES = H // P
BLOCKS = S // P
TWO_PI = 2.0 * math.pi
TINY = 1e-30

PAGES = 5
SUM_LAG = 3
EARLY_BLOCKS = 4
GROUP = 256
CHUNKS = [(c0, GROUP) for c0 in range(0, S - GROUP, GROUP)] + [(S - GROUP, P), (S - P, P)]


def tile_list_mushroom_flush_features_kernel(
    tc, tab_words, tab_scales, tab2_words, tab2_scales, offs, offs2, pos1, wa, ws_words, ws_scales,
    wb, gb, wgs, gz, wo_words, wo_scales, out_0, out_1, out_2,
):
    nc = tc.nc
    with ExitStack() as ctx:
        keep = ctx.enter_context(tc.tile_pool(name="keep", bufs=1))
        psum = ctx.enter_context(tc.psum_pool(name="psum", bufs=1))

        def kept(shape, dtype, name, tag=None):
            return keep.tile(shape, dtype, name=name, tag=tag or name, align_bytes=64)

        def in_turn(items, count):
            return [items[i % len(items)] for i in range(count)]

        banks = [psum.tile([P, BANK], F32, name=f"bank{i}") for i in range(8)]
        sine_banks = in_turn(banks[2:5], 2 * BLOCKS)
        early_banks = in_turn(banks[0:2], 2 * EARLY_BLOCKS)
        late_banks = in_turn(banks[0:5], 2 * (BLOCKS - EARLY_BLOCKS))
        short_banks = in_turn(banks[5:8] + banks[0:2], SLICES)
        sum_banks = in_turn(late_banks[:-6:-1] + banks[5:8], 2 * SLICES)
        y_banks = in_turn(banks[0:5], BLOCKS)

        wide = [kept([P, PACK * BANK], F32, f"wide{i}") for i in range(8)]
        raw_home = {("wb", 0, 0): 0, ("wb", 1, 0): 1, ("wb", 0, 1): 2, ("wb", 1, 1): 3, ("wa", 0, 0): 4, ("wa", 0, 1): 5}
        numer_flat = {(0, 0): wide[0], (0, 1): wide[1], (1, 0): wide[4], (1, 1): wide[5]}
        numer = {key: t[:].rearrange("p (g t c) -> p g t c", t=PACK, c=GROUP) for key, t in numer_flat.items()}
        damp_flat = {(0, 0): wide[6], (0, 1): wide[7], (1, 0): wide[2], (1, 1): wide[3]}
        damp = {key: t[:].rearrange("p (t c) -> p t c", t=PACK) for key, t in damp_flat.items()}
        linear = [kept([P, H], F32, f"linear{jb}") for jb in range(BLOCKS)]
        sine = [kept([P, H], F32, f"sine{jb}") for jb in range(BLOCKS)]
        staging = [kept([P, PACK * BANK], BF16, f"staging{i}") for i in range(3)]
        turns = [kept([P, BANK], I32, f"turns{i}") for i in range(3)]

        idx = keep.tile([P, S // 16], U16, name="idx")
        idx2 = keep.tile([P, NP // 16], U16, name="idx2")
        place = keep.tile([P, NP // 16], U16, name="place")

        def zeroed_plane(width, name):
            plane = kept([P, width], U8, name)
            nc.vector.memset(plane[:].bitcast(I32), 0)
            return plane

        tab_s = zeroed_plane(T, "tab_s")
        ws_s = zeroed_plane(H, "ws_s")
        tab2_s = zeroed_plane(T2, "tab2_s")
        wo_s = zeroed_plane(N, "wo_s")
        pages = [kept([P, S], F32, f"page{i}") for i in range(PAGES)]
        for page in pages:
            nc.vector.memset(page[:].bitcast(I32), 0)
        act_col = kept([P, SLICES], F32, "act_col")
        nc.gpsimd.memset(act_col[:], 0.0)
        nc.scalar.activation(act_col[:], act_col[:], ACT.Sin)
        ident = kept([P, P], F32, "ident")
        make_identity(nc, ident[:])

        def load_planes(plane, scales):
            rows = PACK * scales.shape[0]
            for q in range(4):
                nc.sync.dma_start(
                    out=plane[32 * q : 32 * q + rows, :].bitcast(I32),
                    in_=scales[:, 4 * q : 4 * q + 4, :].bitcast(I32),
                )

        def raw_chunk(key):
            return wide[raw_home[key]][:].rearrange("p (j c) -> p j c", j=PACK)

        def load_weight(key):
            name, a, b = key
            rows = {"wa": wa, "wb": wb}[name][a * BANK : (a + 1) * BANK, b * BANK : (b + 1) * BANK]
            nc.sync.dma_start(out=raw_chunk(key), in_=rows.rearrange("(p j) c -> p j c", j=PACK))

        gb_t = kept([P, 2, PACK], F32, "gb_t")
        gz_t = kept([P, 2, PACK], F32, "gz_t")
        tab_w = kept([P, T], I32, "tab_w", "table_then_y")
        tab2_w = kept([P, 2, T2], I32, "tab2_w", "table2_then_y")
        ws_w = kept([P, 2 * H], U8, "ws_w")
        wo_w = kept([P, 2, N], I32, "wo_w", "wo_then_z")
        wg = kept([P, PACK, NP], F32, "wg")
        weight_order = [("wa", 0, 0), ("wa", 0, 1), ("wb", 0, 0), ("wb", 1, 0), ("wb", 0, 1), ("wb", 1, 1)]

        nc.sync.dma_start(idx[:], offs)
        nc.sync.dma_start(idx2[:], offs2)
        nc.sync.dma_start(place[:], pos1)
        nc.sync.dma_start(out=gb_t[:], in_=gb.rearrange("(b p t) -> p b t", b=2, t=PACK))
        nc.sync.dma_start(out=gz_t[:], in_=gz.rearrange("(b p t) -> p b t", b=2, t=PACK))
        nc.sync.dma_start(out=tab_w[:], in_=tab_words[0].rearrange("p t i -> p (t i)").bitcast(I32))
        for b in range(2):
            cols = slice(b * H, (b + 1) * H)
            nc.sync.dma_start(out=ws_w[:, cols].bitcast(I32), in_=ws_words[0][:, cols].bitcast(I32))
        load_planes(tab_s, tab_scales)
        load_weight(weight_order[0])
        load_planes(ws_s, ws_scales)
        for key in weight_order[1:4]:
            load_weight(key)
        nc.sync.dma_start(out=tab2_w[:], in_=tab2_words.rearrange("a p t i -> p a (t i)").bitcast(I32))
        load_planes(tab2_s, tab2_scales)
        for key in weight_order[4:]:
            load_weight(key)
        for q in range(4):
            nc.sync.dma_start(out=wg[32 * q : 32 * q + 32], in_=wgs.rearrange("(m t) j -> m t j", t=PACK))
        nc.sync.dma_start(out=wo_w[:], in_=wo_words.rearrange("a p c i -> p a (c i)").bitcast(I32))
        load_planes(wo_s, wo_scales)

        sg = kept([P, SLICES], F32, "sg")
        gz_abs = kept([P, SLICES], F32, "gz_abs")
        gz_inv = kept([P, SLICES], F32, "gz_inv")
        gb_sg = kept([P, SLICES], F32, "gb_sg")
        gz_cols = gz_t[:].rearrange("p b t -> p (b t)")
        nc.vector.tensor_scalar(sg[:], gz_cols, 0.0, 2.0, ALU.is_ge, ALU.mult)
        nc.vector.tensor_scalar(sg[:], sg[:], -1.0, None, ALU.add)
        nc.vector.tensor_tensor(gz_abs[:], gz_cols, sg[:], ALU.mult)
        nc.vector.tensor_tensor(gb_sg[:], gb_t[:].rearrange("p b t -> p (b t)"), sg[:], ALU.mult)
        nc.vector.tensor_scalar_max(gz_abs[:], gz_abs[:], TINY)
        nc.vector.reciprocal(gz_inv[:], gz_abs[:])

        v_w = kept([P, S], U32, "v_w", "v_then_y")
        v_s = kept([P, S], U8, "v_s")
        v2_w = kept([P, 2, NP], U32, "v2_w", "v2_then_z")
        v2_s = kept([P, NP], U8, "v2_s")
        for h in range(2):
            cols = slice(h * BANK, (h + 1) * BANK)
            entries = idx[:, h * BANK // 16 : (h + 1) * BANK // 16]
            nc.vector.tensor_copy(v_w[:, cols], tab_w[:].bitcast(U32).indirect(entries))
            nc.vector.tensor_copy(v_s[:, cols], tab_s[:].indirect(entries))

        quantised = {}

        def quantise_weight(n):
            key = weight_order[n]
            grouped = staging[n % len(staging)]
            dst = grouped[:].rearrange("p (u v m j) -> p u m j v", u=2, v=2, j=PACK)
            src = raw_chunk(key).rearrange("p j (m u v) -> p u m j v", u=2, v=2)
            if n == len(weight_order) - 1:
                nc.vector.tensor_copy(dst, src)
            else:
                nc.scalar.copy(dst, src)
            codes = kept([P, BANK], U32, f"codes{n}")
            scales = kept([P, BANK], U8, f"scales{n}")
            nc.vector.quantize_mx(out=codes[:].bitcast(FP8X4), scales=scales[:], in_=grouped[:])
            quantised[key] = (codes, scales)

        def dealt(ap):
            return ap.rearrange("p (m t) -> p t m", t=PACK)

        def by_slices(ap):
            return ap.rearrange("p (t m) -> p t m", t=PACK)

        def count_turns(i):
            jb, b = divmod(i, 2)
            js = slice(jb * P, (jb + 1) * P)
            nc.tensor.matmul_mx(
                out=sine_banks[i][:], lhsT=v_w[:, js].bitcast(FP8X4), lhsT_scale=v_s[:, js],
                rhs=ws_w[:, 2 * b * BANK : 2 * (b + 1) * BANK].bitcast(FP4X4),
                rhs_scale=ws_s[:, b * BANK : (b + 1) * BANK], start=True, stop=True,
            )
            nc.vector.tensor_scalar(by_slices(turns[i % 3][:]), dealt(sine_banks[i][:]), 1.0 / TWO_PI, None, ALU.mult)

        def take_sine(i):
            jb, b = divmod(i, 2)
            dst = sine[jb][:, b * BANK : (b + 1) * BANK]
            nc.vector.scalar_tensor_tensor(
                by_slices(dst), by_slices(turns[i % 3][:]), -TWO_PI, dealt(sine_banks[i][:]), ALU.mult, ALU.add
            )
            nc.scalar.activation(dst, dst, ACT.Sin, bias=act_col[:, 0:1])

        def linear_part(jb):
            js = slice(jb * P, (jb + 1) * P)
            for b in range(2):
                bank = (early_banks + late_banks)[2 * jb + b]
                codes, scales = quantised["wa", 0, b]
                nc.tensor.matmul_mx(
                    out=bank[:], lhsT=v_w[:, js].bitcast(FP8X4), lhsT_scale=v_s[:, js],
                    rhs=codes[:].bitcast(FP8X4), rhs_scale=scales[:], start=True, stop=True,
                )
                nc.scalar.copy(linear[jb][:, b * BANK : (b + 1) * BANK], bank[:])

        count_turns(0)
        for jb in range(BLOCKS):
            for i in (2 * jb, 2 * jb + 1):
                if i + 1 < 2 * BLOCKS:
                    count_turns(i + 1)
                take_sine(i)
            if 1 <= jb <= len(weight_order):
                quantise_weight(jb - 1)
            if 2 <= jb < 2 + EARLY_BLOCKS:
                linear_part(jb - 2)
            if jb == BLOCKS // 2:
                for a in range(2):
                    nc.vector.tensor_copy(v2_w[:, a, :], tab2_w[:, a, :].bitcast(U32).indirect(idx2[:]))
                nc.vector.tensor_copy(v2_s[:], tab2_s[:].indirect(idx2[:]))

        wo_dealt_w = kept([P, 2, N], I32, "wo_dealt_w")
        wo_dealt_s = kept([P, N], U8, "wo_dealt_s")
        nc.vector.tensor_copy(
            wo_dealt_w[:].rearrange("p a (u v m) -> p a u m v", u=2, v=2),
            wo_w[:].rearrange("p a (m u v) -> p a u m v", u=2, v=2),
        )
        nc.vector.tensor_copy(by_slices(wo_dealt_s[:]), dealt(wo_s[:]))

        nc.scalar.copy(act_col[:], gz_inv[:])

        short_homes = [turns[(2 * BLOCKS + s) % 3][:].bitcast(F32) for s in range(-3, 0)]
        short_homes += [numer_flat[0, (s - 3) % 2][:, (s - 3) * GROUP : (s - 1) * GROUP] for s in range(3, 6)]
        short_homes += [numer_flat[1, 0][:, 0:NP], staging[0][:].bitcast(F32)[:, 0:NP]]

        def short_product(s):
            b, t = divmod(s, PACK)
            ms = slice(t * P, (t + 1) * P)
            for a in range(2):
                codes, scales = quantised["wb", a, b]
                nc.tensor.matmul_mx(
                    out=short_banks[s][:], lhsT=codes[:, ms].bitcast(FP8X4), lhsT_scale=scales[:, ms],
                    rhs=v2_w[:, a, :].bitcast(FP8X4), rhs_scale=v2_s[PACK * a : P, :], start=(a == 0), stop=(a == 1),
                )
            nc.scalar.activation(short_homes[s], short_banks[s][:], ACT.Copy, scale=gb_sg[:, s : s + 1])

        def damping(s, halves):
            b, t = divmod(s, PACK)
            col = act_col[:, s : s + 1]
            for h in halves:
                nc.scalar.activation(damp[b, h][:, t, :], pages[s % PAGES][:, h * BANK : (h + 1) * BANK], ACT.Abs)
            for h in halves:
                nc.scalar.activation(
                    damp[b, h][:, t, :], damp[b, h][:, t, :], ACT.Abs_reciprocal_sqrt, scale=col, bias=col
                )
            for h in halves:
                nc.scalar.activation(damp[b, h][:, t, :], damp[b, h][:, t, :], ACT.Square)

        def numerator(s):
            b, t = divmod(s, PACK)
            rs = slice(s * P, (s + 1) * P)
            for h in range(2):
                bank = sum_banks[2 * s + h]
                for c in range(BANK // P):
                    dst = bank[:, c * P : (c + 1) * P]
                    jb = h * BANK // P + c
                    nc.tensor.matmul(dst, linear[jb][:, rs], ident[:], start=True, stop=False, is_transpose=True)
                    nc.tensor.matmul(dst, sine[jb][:, rs], ident[:], start=False, stop=True, is_transpose=True)
                nc.vector.scalar_tensor_tensor(
                    numer[b, h][:, :, t, :], bank[:].rearrange("p (g c) -> p g c", c=GROUP), sg[:, s : s + 1],
                    pages[s % PAGES][:, h * BANK : (h + 1) * BANK].rearrange("p (g c) -> p g c", c=GROUP),
                    ALU.mult, ALU.add,
                )

        for s in range(SLICES):
            short_product(s)
        for jb in range(EARLY_BLOCKS, BLOCKS):
            linear_part(jb)
        for s in range(SLICES):
            nc.vector.tensor_tensor(pages[s % PAGES][:].indirect(place[:]), short_homes[s], wg[:, s % PACK, :], ALU.mult)
            if s < SLICES - 1:
                damping(s, (0, 1))
            else:
                damping(s, (0,))
                damping(s, (1,))
            if s >= SUM_LAG:
                numerator(s - SUM_LAG)
        for s in range(SLICES - SUM_LAG, SLICES):
            numerator(s)

        z_w = [kept([P, S], U32, "z_w0", "wo_then_z"), kept([P, S], U32, "z_w1", "v2_then_z")]
        z_s = [kept([P, S], U8, f"z_s{b}") for b in range(2)]
        y_w = kept([P, S], I32, "y_w", "v_then_y")
        y_s = kept([P, S], U8, "y_s")
        y_f32 = [kept([P, PACK, BANK], F32, "y_f32_0", "table2_then_y"), kept([P, PACK, BANK], F32, "y_f32_1", "table_then_y")]
        y_bf16 = [linear[h][:].bitcast(BF16) for h in range(2)]
        y_rows = out_0.rearrange("(p t) j -> p t j", t=PACK)
        y_codes = out_1[0].rearrange("p m t -> p (m t)").bitcast(I32)

        def z_home(n, b):
            c0, width = CHUNKS[n]
            if b == 1:
                return staging[1 + n % 2][:, 0 : PACK * width]
            if n == 0:
                return staging[0][:, 0 : PACK * width]
            h, g = divmod(c0 // GROUP - 1, 2)
            spent = numer_flat[1, h][:, g * PACK * GROUP : (g + 1) * PACK * GROUP].bitcast(BF16)
            return spent[:, PACK * (c0 % GROUP) : PACK * (c0 % GROUP + width)]

        def features(n, b):
            c0, width = CHUNKS[n]
            h, off = divmod(c0, BANK)
            g, first = divmod(off, GROUP)
            cols = slice(c0, c0 + width)
            zb = z_home(n, b)
            nc.vector.tensor_tensor(
                zb.rearrange("p (c i t) -> p c t i", i=2, t=PACK),
                numer[b, h][:, g, :, first : first + width].rearrange("p t (c i) -> p c t i", i=2),
                damp[b, h][:, :, off : off + width].rearrange("p t (c i) -> p c t i", i=2),
                ALU.mult,
            )
            nc.vector.quantize_mx(out=z_w[b][:, cols].bitcast(FP8X4), scales=z_s[b][:, cols], in_=zb)

        def last_product(n):
            c0, width = CHUNKS[n]
            h, off = divmod(c0, BANK)
            cols = slice(c0, c0 + width)
            plain = y_f32[h][:, :, off : off + width]
            woven = y_bf16[h][:, PACK * off : PACK * (off + width)]
            for c in range(width // P):
                js = slice(c0 + c * P, c0 + (c + 1) * P)
                bank = y_banks[c0 // P + c][:].rearrange("p (t n) -> p t n", t=PACK)
                for t in range(PACK):
                    ms = slice(t * P, (t + 1) * P)
                    for b in range(2):
                        nc.tensor.matmul_mx(
                            out=bank[:, t, :], lhsT=wo_dealt_w[:, b, ms].bitcast(FP8X4),
                            lhsT_scale=wo_dealt_s[PACK * b : P, ms],
                            rhs=z_w[b][:, js].bitcast(FP8X4), rhs_scale=z_s[b][:, js], start=(b == 0), stop=(b == 1),
                        )
                dst = woven.rearrange("p (n t) -> p n t", t=PACK)[:, c * P : (c + 1) * P, :]
                if n == len(CHUNKS) - 1:
                    nc.vector.tensor_copy(dst, bank.rearrange("p t n -> p n t"))
                else:
                    nc.scalar.copy(dst, bank.rearrange("p t n -> p n t"))
                nc.scalar.copy(plain[:, :, c * P : (c + 1) * P], bank)
            nc.vector.quantize_mx(out=y_w[:, cols].bitcast(FP8X4), scales=y_s[:, cols], in_=woven)
            nc.sync.dma_start(out=y_rows[:, :, cols], in_=plain)
            if (c0 + width) % BANK == 0:
                half = slice(h * BANK, (h + 1) * BANK)
                nc.sync.dma_start(out=y_codes[:, half], in_=y_w[:, half])

        for n in range(len(CHUNKS)):
            features(n, 0)
            features(n, 1)
            last_product(n)
        for q in range(4):
            nc.sync.dma_start(
                out=out_2[0, 4 * q : 4 * q + 4, :].bitcast(I32), in_=y_s[32 * q : 32 * q + 4, :].bitcast(I32)
            )
